import numpy as np, ml_dtypes
CORES = [24,25,26,27,28,29,30,31]
N = 8
import mx_ref
BF = ml_dtypes.bfloat16
def entries(a):
    return np.ascontiguousarray(a.T).reshape(-1)
def table(e):
    return np.ascontiguousarray(np.reshape(e, (-1, 16)).T).astype(np.int32)
def gentries(a):
    return np.ascontiguousarray(a.reshape(8, 16, -1).transpose(0, 2, 1)).reshape(8, -1)
def gtable(e):
    e = np.asarray(e); return np.ascontiguousarray(e.reshape(8, -1, 16).transpose(0, 2, 1)).reshape(128, -1).astype(np.int32)
def gcols(t, e):
    v = np.concatenate([t.reshape(8, 16, -1, 4), np.zeros((8, 16, 1, 4), BF)], axis=2)
    return np.ascontiguousarray(np.stack([v[g][:, e[g]] for g in range(8)])).reshape(128, -1)
def tile(rs):
    return np.stack(rs, axis=2).reshape(128, -1).astype(BF)
def pick(q, e):
    c = np.concatenate([q[0].reshape(128, -1, 4), np.zeros((128, 1, 4), np.uint8)], axis=1); s = np.concatenate([q[1], np.ones((16, 1), np.uint8)], axis=1)
    return (np.ascontiguousarray(c[:, e].reshape(128, -1)), np.ascontiguousarray(s[:, e]))
def join(*qs):
    return (np.concatenate([q[0] for q in qs], axis=1), np.concatenate([q[1] for q in qs], axis=1))
def put(q, e, v):
    c, s = q[0].reshape(128, -1, 4).copy(), q[1].copy(); c[:, e] = v[0].reshape(128, -1, 4); s[:, e] = v[1]
    return (c.reshape(128, -1), s)
def pk(c, s):
    return (np.ascontiguousarray(c), mx_ref.live(s))
def emit(q):
    return q[0], q[1]
def packed(v, rng):
    q = [mx_ref.quantize(np.ascontiguousarray(v[r])) for r in range(N)]
    return np.stack([a for a, b in q]), np.stack([mx_ref.plane(b, rng) for a, b in q])
def values_of_codes():
    e, c = np.zeros((128, 128, 4), np.float32), np.zeros((128, 2, 4), np.uint8)
    e[np.arange(128), np.arange(128), 0] = 1
    c[:127, :, 0] = np.arange(256).reshape(2, 128).T[:127]
    return mx_ref.matmul(mx_ref.quantize(e.reshape(128, 512).astype(BF)), (c.reshape(128, 8), np.full((16, 2), 127, np.uint8))).T.reshape(-1).astype(np.float64)
CODE_VALUE, SCALE_VALUE = values_of_codes(), 2.0 ** (np.arange(256) - 127.0)
def decode(q):
    return (CODE_VALUE[q[0]].reshape(16, 8, -1, 4) * SCALE_VALUE[q[1]][:, None, :, None] + 0.0).reshape(128, -1).astype(np.float32)
def f(rng, *shape):
    return mx_ref.flush((rng.standard_normal(shape, dtype=np.float32) * np.exp2(rng.integers(-2, 3, shape[:-1] + (1,)))).astype(BF))
def wide(rng, *shape, cols=0):
    v = rng.standard_normal(shape, dtype=np.float32) * np.exp2(rng.integers(-12, 13, shape)).astype(np.float32)
    if cols: v *= np.repeat(np.exp2(rng.integers(-cols, cols + 1, shape[:-2] + (1, shape[-1] // 4))) * (rng.random(shape[:-2] + (1, shape[-1] // 4)) > 0.0625), 4, axis=-1).astype(np.float32)
    return mx_ref.flush(v.astype(BF))
C = 384
STEP = [1, 2, 4]
def numbers_of(rng):
    return {"x": np.array(f(rng, N, 128, 4 * C)), "u": np.array(f(rng, N, 128, 512)), "v": np.array(f(rng, N, 128, 512))}
def orders(rng):
    return rng.permuted(np.tile(np.arange(C), (N, 1)), axis=1)
def pairing(rng):
    p = rng.permuted(np.tile(np.arange(C), (N, 8, 1)), axis=2)
    m = np.zeros((N, 8, C), np.int64)
    np.put_along_axis(m, p[:, :, ::2], p[:, :, 1::2], axis=2)
    np.put_along_axis(m, p[:, :, 1::2], p[:, :, ::2], axis=2)
    return m
def stored(a, t, m):
    return {"la": np.stack([table(a[r]) for r in range(N)]), "lb": np.stack([table(t[r]) for r in range(N)]), "mt": np.stack([gtable(m[r]) for r in range(N)])}
def lists(rng):
    return stored(orders(rng), orders(rng), pairing(rng))
def layers(rng, still=[]):
    w = np.array(f(rng, N, 128, 2048)).reshape(N, 8, 16, 4, 8, 16, 4)
    for i in still:
        w[:, :, i] = 0
        w[:, :, :, :, :, i] = 0
    return w
def weights(rng, w):
    c, p = packed(np.ascontiguousarray(w).reshape(N, 128, 2048), rng)
    return {"wc": c, "ws": p}
def setup_inputs(rng):
    return {**numbers_of(rng), **lists(rng), **weights(rng, layers(rng))}
def setup_inputs_ties(rng):
    d = numbers_of(rng)
    m = pairing(rng)
    o = rng.permutation(N)
    k = rng.integers(0, 4, (N, 8, C))
    k[o[1]] += 1
    k[o[2]] = (np.arange(C) > m[o[2]]) == (rng.permutation(8) < 4)[:, None]
    k[o[3]] = 1
    h = rng.permutation(8)
    k[o[3], h[:4], C - 1] = 2
    k[o[3], h[4:], 0] = 0
    x = d["x"].reshape(N, 8, 16, C, 4)
    x[:, :, 0] = 0
    x[:, :, 0, :, 0] = k.astype(np.float32).astype(BF)
    a = np.tile(np.exp2(rng.integers(-3, 4, (1, 8, 1)).astype(np.float32)), (N, 1, C))
    x[:, :, 8:] = 0
    x[:, :, 8, :, 0] = (-1.125 * a).astype(BF)
    x[:, :, 10, :, 0] = (-0.0703125 * a).astype(BF)
    u = d["u"].reshape(N, 128, 128, 4)
    u[:, :, ::16] = 0
    for r in range(N):
        for i in range(0, 128, 16): u[r, i, i, 0] = 0.0 if r == o[0] else -1.0 if r == o[1] else 1.0
    w = layers(rng, [0])
    w[:, :, :, :, :, 8:] = 0
    for g in range(8):
        w[:, g, 8, 0, g, 8, 0] = -28.0
        for b in range(4): w[:, g, 10, b, g, 9, 0] = -2.0 ** (b - 5)
    return {"x": x.reshape(N, 128, 4 * C), "u": u.reshape(N, 128, 512), "v": d["v"], **stored(orders(rng), orders(rng), m), **weights(rng, w)}
def setup_inputs_near(rng):
    d = numbers_of(rng)
    o = np.zeros(N, np.int64)
    for n, r in enumerate(rng.permutation([r for r in range(N) if r < r ^ STEP[0]])):
        e = rng.integers(2)
        o[r], o[r ^ STEP[0]] = n % 2 * 2 + e, n % 2 * 2 + 1 - e
    x = d["x"].astype(np.float32).reshape(N, 8, 16, C, 4)
    x[:, :, 0] = 0
    x[:, :, 8:] = 0
    u = d["u"].reshape(N, 128, 128, 4)
    u[:, :, ::16] = 0
    w = layers(rng, [0, 1, 8, 9, 10, 11, 12, 13, 14, 15])
    for r in range(N):
        c = rng.choice([-1.0, 1.0], (8, 1))
        s = rng.integers(0, 16, (8, C))
        digits = ((s[:, :, None] >> np.arange(4)) & 1) * np.exp2(np.arange(4) - 23.0)
        if o[r] < 2:
            x[r, :, 0, :, 0] = c
            x[r, :, 8] = digits
            x[r, :, 11, :, 0] = 2.0 ** -10
        elif o[r] == 2:
            x[r, :, 8] = digits * rng.choice([-1.0, 1.0], (8, C, 1))
            x[r, :, 1:8] = 0
            x[r, :, 1, :, 0] = rng.choice([-1.0, 1.0], (8, C)) * 2.0 ** -30
            for g in range(8):
                w[r, g, 1, 0, g, 12, 0] = 2.0 ** -8
                w[r, g, 1, 0, g, 13, 0] = 64.0
        else:
            x[r, :, 8, :, 0] = np.where(s < 8, 1.25, 0.0) * 2.0 ** -30 * c
            x[r, :, 9, :, 0] = np.where(s < 8, 0.0, 1.125) * 2.0 ** -30 * c
            for g in rng.permutation(8)[:4]:
                e = rng.choice([-1.0, 1.0], C) * 2.0 ** -30
                x[r, g, 8, :, 0] = 1.25 * e
                x[r, g, 9, :, 0] = -1.125 * e
        at = [0, C - 1, int(rng.integers(C)), int(rng.integers(C))]
        for g, j in zip(rng.permutation(8)[:4], at): x[r, g, 0, j, 0] = 2.0 ** 29 * rng.choice([-1.0, 1.0])
        k = 1.0 if o[r] == 0 else 2.0 ** -30
        for h in range(0, 128, 16):
            u[r, h, h, 0] = k
            if o[r] < 2: u[r, h + 11, h, 0] = k
            if o[r] < 3: u[r, h + 8, h] = k
            else:
                u[r, h + 8, h, 0] = k
                u[r, h + 9, h, 0] = 1.125 * k
                u[r, h + 12, h, 0] = k
    return {"x": x.reshape(N, 128, 4 * C).astype(BF), "u": u.reshape(N, 128, 512), "v": d["v"], **lists(rng), **weights(rng, w)}
def setup_inputs_odd(rng):
    d = numbers_of(rng)
    x = (1.0 + (2 * rng.integers(0, 64, (N, 16, 8, C, 4)) + 1) * 2.0 ** -7) * np.exp2(-rng.integers(0, 7, (N, 16, 8, C, 4)).astype(np.float64)) * rng.choice([-1.0, 1.0], (N, 16, 8, C, 4))
    x[:, :, 0, :, 0] = 1.96875 * 2.0 ** 8 * rng.choice([-1.0, 1.0], (N, 16, C))
    u = d["u"].reshape(N, 16, 8, 128, 4)
    u[:, :, 0, ::16] = 0
    for r in range(N):
        for n, g in enumerate(rng.permutation(8)[:4]):
            x[r, 2 * g, 1, :, 0] = (8 + rng.integers(0, 2, C)) * 2.0 ** (n % 2 - 8)
            u[r, :, :, 16 * g] = 0
            u[r, 2 * g, 1, 16 * g, 0] = 1.0
    return {"x": x.astype(np.float32).reshape(N, 128, 4 * C).astype(BF), "u": u.reshape(N, 128, 512), "v": d["v"], **lists(rng), **weights(rng, layers(rng, [0, 8]))}
def setup_inputs_ends(rng):
    d = numbers_of(rng)
    o, e = rng.permutation(N) % 4, rng.permutation(N) % 4
    x = np.zeros((N, 8, 16, C, 4))
    u = d["u"].astype(np.float32).reshape(N, 128, 128, 4)
    v = np.zeros((N, 128, 512))
    w = np.zeros((N, 128, 4, 128, 4), np.float32)
    still = int(rng.integers(8))
    i = np.arange(128)
    for r in range(N):
        h = rng.permutation(8)
        c = np.where(h < 2, 0.0, h % 2 * 2.0 - 1.0)[None, :, None]
        large = (0.88 + 0.04 * rng.random((8, 16, C, 4))) * 2.0 ** 30
        if o[r] == 0: x[r] = -large
        if o[r] == 1: x[r] = large * rng.choice([-1.0, 1.0], (C, 1))
        if o[r] == 2: x[r] = -(1.0 + 0.125 * rng.integers(0, 8, (8, 16, C, 4))) * 2.0 ** -30
        if o[r] == 3: x[r] = d["x"][r].astype(np.float32).reshape(8, 16, C, 4)[:, :, :1]
        if o[r] < 2: u[r, :, ::16] = c * (0.9 + 0.1 * rng.random((128, 8, 4))) * 2.0 ** 30
        if o[r] == 2: u[r, :, ::16] = c * (1.0 + 0.125 * rng.integers(0, 8, (128, 8, 4))) * 2.0 ** -30
        if o[r] == 3: u[r, :, ::16] *= np.abs(c).astype(np.float32)
        v[r] = rng.choice([-1.0, 1.0], (128, 512)) * (2.0 ** 30 if o[r] < 2 else 2.0 ** -30)
        k = np.array([0.125, 0.25, 0.5])[rng.permutation(8) % 3]
        if o[r] == 2: k[:] = 32.0
        if o[r] == 3: k[k == 0.125] = 2.0 ** -8
        k[still] = 256.0 if o[r] == 2 else 0.0
        for b in range(4): w[r, i, b, i, b] = k[i // 16]
    a, t, m = orders(rng), orders(rng), pairing(rng)
    j = np.arange(C)
    a[e == 0] = j
    t[e == 0] = j
    m[e == 0] = j ^ 1
    a[e == 1] = C - 1 - j
    t[e == 1] = C - 1 - j
    m[e == 1] = C - 1 - j
    a[e == 2] = (j + 1) % C
    t[e == 2] = (j + C - 1) % C
    m[e == 2] = (j + C // 2) % C
    return {"x": x.astype(np.float32).reshape(N, 128, 4 * C).astype(BF), "u": u.reshape(N, 128, 512).astype(BF), "v": v.astype(np.float32).astype(BF), **stored(a, t, m), **weights(rng, w.astype(BF))}
def setup_inputs_spread(rng):
    d = setup_inputs(rng)
    d["x"] = wide(rng, N, 128, 4 * C, cols=6)
    return d
def check_inputs(d):
    b = []
    for k in ("x", "u", "v"):
        a = np.abs(d[k].astype(np.float32))
        if not (np.isfinite(a).all() and ((a == 0) | (a >= 2.0 ** -30) & (a <= 2.0 ** 30)).all()): b.append("a value of " + k)
    none, least, most = [emit(mx_ref.quantize(np.full((128, 16), k, np.float32).astype(BF)))[1][0, 0] for k in (0.0, 2.0 ** -8, 2.0 ** 8)]
    for r in range(N):
        for k in ("la", "lb"):
            if (np.sort(entries(d[k][r])) != np.arange(C)).any(): b.append(k + ": not every number once")
        m = gentries(d["mt"][r])
        if not ((m >= 0) & (m < C)).all(): b.append("an entry of mt")
        elif (np.take_along_axis(m, m, axis=1) != np.arange(C)).any() or (m == np.arange(C)).any(): b.append("mt: not in pairs")
        if ((d["wc"][r] == 0x7F) | (d["wc"][r] == 0xFF)).any(): b.append("wc: a code that is no number")
        s = mx_ref.live(d["ws"][r])
        if ((s != none) & ((s < least) | (s > most))).any(): b.append("ws: a scale out of range")
        if (((d["wc"][r].reshape(16, 8, 512, 4) & 0x7F) != 0) & (s == none)[:, None, :, None]).any(): b.append("wc: a code other than zero under the scale of zeros")
    return b
def reference(x, u, v, la, lb, mt, wc, ws):
    qu = [mx_ref.quantize(u[r]) for r in range(N)]
    lay = [pk(wc[r], ws[r]) for r in range(N)]
    mate = [gentries(mt[r]) for r in range(N)]
    kept = [[entries(la[r]), entries(lb[r])] for r in range(N)]
    now = [x[r] for r in range(N)]
    here = np.tile(np.arange(C), (8, 1))
    ll = np.zeros((N, 8, C), np.float32)
    for step in STEP:
        went, sent = [], []
        for r in range(N):
            s = mx_ref.matmul(qu[r], mx_ref.quantize(now[r]))[::16] + np.float32(0.0)
            t = np.take_along_axis(s, mate[r], axis=1)
            crossed = np.where(here < mate[r], s < t, t < s)
            e = np.where(crossed, mate[r], here)
            a = [kept[r][0][e[0]], kept[r][1][e[7]]]
            kept[r] = a[:2]
            for g in range(1, 7):
                k = e[g][a[g]]
                a.append(a[g - 1][k[k]])
            went.append(np.stack(a))
            ll[r] = went[r]
            z = mx_ref.quantize(gcols(now[r], went[r]))
            sent.append(mx_ref.quantize(tile([mx_ref.matmul(pick(lay[r], np.arange(128 * b, 128 * b + 128)), z) * np.float32(0.03125) for b in range(4)])))
        made = []
        for r in range(N):
            far = gcols(decode(sent[r ^ step]).astype(BF), went[r][::-1])
            made.append((now[r].astype(np.float32) + far.astype(np.float32)).astype(BF))
        now = made
    y = np.zeros((N, 128, C), np.float32)
    oc, osc = np.zeros((N, 128, 4 * C), np.uint8), np.zeros((N, 16, C), np.uint8)
    for r in range(N):
        q = mx_ref.quantize(now[r])
        y[r] = mx_ref.matmul(mx_ref.quantize(v[r]), q)
        oc[r], osc[r] = emit(q)
    return {"y": y, "ll": ll, "oc": oc, "osc": osc}

@@ -1,0 +1,495 @@
+from concourse.mybir import dt, AluOpType as OP, ActivationFunctionType as AF
+
+C = 384
+HALF = C // 2
+SCH = [(0, HALF), (HALF, C)]
+ZCH = [(0, 128), (128, 256), (256, 384)]
+NCH = [(0, 128), (128, 256), (256, 400)]
+STEP = [1, 2, 4]
+ROW = 416
+NV = 12
+
+SCRATCH = {}
+SEMAPHORES = ["cv", "cs", "ct", "cg", "are", "loe"]
+
+
+def _declare():
+    def sb(name, cols, dtype):
+        SCRATCH[name] = ("sbuf", [128, cols], dtype)
+    bf, f32, i32, u16, co, u8 = "bfloat16", "float32", "int32", "uint16", "float8_e4m3fn_x4", "uint8"
+    for n, c in (("xt", 4 * C), ("ut", 512), ("vt", 512), ("zt", 4 * C), ("hg", 4 * C), ("fl", 4 * ROW), ("ones", 512), ("onem", 512), ("c0", 512),
+                 ("ce", 512), ("cd", 512), ("e0", 512), ("e1", 512), ("e2", 512), ("e3", 512), ("r0", C), ("r0c", C), ("newc", 400), ("idc", C), ("base", 400),
+                 ("new", ROW), ("pa", ROW), ("tr", 8 * ROW), ("lb16", C)):
+        sb(n, c, bf)
+    for b in range(4):
+        sb("xp%d" % b, C, bf)
+        sb("hp%d" % b, C, bf)
+    for k in range(8):
+        sb("f%d" % k, ROW, bf)
+    for n, c in (("idf", 400), ("wsg", C), ("wf", C), ("dl8", C), ("delta", 400), ("tm", 400), ("dab", 400), ("sw", C), ("ns", C), ("ysb", C), ("l32", C),
+                 ("cb", 1), ("cn", 1), ("cm", 1), ("p15", 1), ("c32", 1), ("bs1", 1), ("t1", 1), ("t2", 1), ("t3", 1), ("bs2", 1), ("k2", 2)):
+        sb(n, c, f32)
+    for n, c in (("mti", 24), ("offi", 24), ("ip", 1), ("b16", 1), ("i15", 1), ("ph", 1), ("ik", 2), ("mi", 26)):
+        sb(n, c, i32)
+    for n, c in (("mt16", 24), ("offa", 24), ("sel", 6), ("ml", 26), ("oa", 26), ("ob", 26), ("lf", 96), ("le", 24), ("lm", 24)):
+        sb(n, c, u16)
+    for k in range(1, 7):
+        sb("ok%d" % k, 26, u16)
+    for n, c in (("xq", C), ("uq", 128), ("vq", 128), ("zq", C), ("hq", C), ("fq", ROW), ("wq", 512), ("ceq", 128), ("cdq", 128),
+                 ("e0q", 128), ("e1q", 128), ("e2q", 128), ("e3q", 128)):
+        sb(n, c, co)
+        sb(n + "s", c, u8)
+    for r in range(3):
+        sb("lr%d" % r, 24, u16)
+        sb("hr%d" % r, C, co)
+        sb("hr%ds" % r, C, u8)
+    for k in range(8):
+        SCRATCH["ps%d" % k] = ("psum", [128, 512], f32)
+    for r in range(3):
+        for n in ("l", "c0", "s0", "c1", "s1"):
+            SEMAPHORES.append("ar%d%s" % (r, n))
+            SEMAPHORES.append("lo%d%s" % (r, n))
+    for n in ("x0", "x1", "mt", "u", "v", "la", "wc", "ws", "mi", "fl", "bs", "dl", "st", "out"):
+        SEMAPHORES.append("d_" + n)
+    for r in range(2):
+        SEMAPHORES.append("d_nb%d" % r)
+        SEMAPHORES.append("d_nd%d" % r)
+
+
+_declare()
+
+
+def _span(a, b, s):
+    return slice(a, b) if s == 1 else slice(a, b, s)
+
+
+def _meet(a0, a1, s, b0, b1, t):
+    if a0 >= b1 or b0 >= a1:
+        return False
+    return not (s == t and s > 1 and (a0 - b0) % s)
+
+
+def _builder(g, T):
+    eng = {"v": g.vector, "s": g.scalar, "t": g.tensor, "g": g, "y": g.sync}
+    known = {q: {} for q in eng}
+    hist, cnt, closed = {}, {}, set()
+    serial = [0]
+
+    def ap(r):
+        name, c, p, bits = r
+        p = slice(None) if p == (0, 128, 1) else _span(*p)
+        a = T[name][p, _span(*c)]
+        return a.bitcast(dt.uint8) if bits else a
+
+    def deps(q, reads, writes, matmul=False):
+        found = {}
+        for refs, w in ((reads, False), (writes, True)):
+            for name, c, p, bits in refs:
+                psum = name[:2] == "ps"
+                for (c2, p2, w2, tok, clk, q2, n) in hist.get(name, ()):
+                    if psum:
+                        if q2 == q and (q == "t" or not (w or w2)):
+                            continue
+                    else:
+                        if not (w or w2):
+                            continue
+                        if not (_meet(*c, *c2) and _meet(*p, *p2)):
+                            continue
+                    found[n] = (tok, clk)
+        return [found[n] for n in sorted(found, reverse=True)]
+
+    def wait(q, toks):
+        k = known[q]
+        for (sem, val), clk in toks:
+            if sem in closed or sem[:2] == "d_":
+                val = cnt[sem]
+                closed.add(sem)
+            if k.get(sem, 0) >= val:
+                continue
+            eng[q].wait_ge(T.sem[sem], val)
+            k[sem] = val
+            for s2, v2 in clk.items():
+                if k.get(s2, 0) < v2:
+                    k[s2] = v2
+
+    def note(q, reads, writes, tok):
+        serial[0] += 1
+        clk = dict(known[q])
+        for refs, w in ((reads, False), (writes, True)):
+            for name, c, p, bits in refs:
+                h = hist.setdefault(name, [])
+                if w and name[:2] != "ps":
+                    h[:] = [e for e in h if not (c[0] <= e[0][0] and e[0][1] <= c[1] and c[2] == 1 and p == (0, 128, 1))]
+                h.append((c, p, w, tok, clk, q, serial[0]))
+
+    def issue(q, fn, reads, writes, sem=None, inc=1):
+        wait(q, deps(q, reads, writes))
+        sem = sem or "c" + q
+        assert sem not in closed, sem
+        cnt[sem] = cnt.get(sem, 0) + inc
+        fn(eng[q]).then_inc(T.sem[sem], inc)
+        note(q, reads, writes, (sem, cnt[sem]))
+
+    def remote(out, src, dst, ars, los, topo, core):
+        wait("g", deps("g", [src], []))
+        rid, pid, _ = topo.addr(dst)
+        n = len(topo.engines(core, dst))
+        g.remote_dma(ap(out), ap(src), T.sem[ars], T.sem[los], pid, rid, topo.mask(core, dst))
+        cnt[los] = n
+        note("g", [src], [], (los, n))
+
+    def arrives(out, sem, n):
+        serial[0] += 1
+        cnt[sem] = n
+        hist.setdefault(out[0], []).append((out[1], out[2], True, (sem, n), {}, "remote", serial[0]))
+
+    def finish():
+        for sem in sorted(cnt):
+            if known["g"].get(sem, 0) < cnt[sem]:
+                g.wait_ge(T.sem[sem], cnt[sem])
+                known["g"][sem] = cnt[sem]
+
+    return ap, issue, remote, arrives, finish
+
+
+def rank_program(g, core, T, topo):
+    rank = T.rank_of(core)
+    if rank is None:
+        return
+    ap, issue, remote, arrives, finish = _builder(g, T)
+
+    def R(name, c0, c1, cs=1, p0=0, p1=128, ps=1):
+        return (name, (c0, c1, cs), (p0, p1, ps), False)
+
+    def B(name, c0, c1):
+        return (name, (c0, c1, 1), (0, 128, 1), True)
+
+    def P(name, p0=0, p1=128):
+        return R(name, 0, 1, 1, p0, p1)
+
+    def dma(q, sem, out, in_, ext_in=None, ext_out=None):
+        issue(q, lambda e: e.dma_start(ext_out if ext_out is not None else ap(out), ext_in if ext_in is not None else ap(in_)),
+              [in_] if in_ else [], [out] if out else [], "d_" + sem, 16)
+
+    def val(s):
+        return ap(s) if isinstance(s, tuple) else s
+
+    def memset(r, c):
+        issue("v", lambda e: e.memset(ap(r), c), [], [r])
+
+    def tt(out, a, b, op, off=None):
+        def fn(e):
+            x = ap(a)
+            return e.tensor_tensor(ap(out), x.indirect(ap(off)) if off else x, ap(b), op)
+        issue("v", fn, [a, b] + ([off] if off else []), [out])
+
+    def ts(out, a, s1, s2, op0, op1=None, off=None):
+        def fn(e):
+            x = ap(a)
+            x = x.indirect(ap(off)) if off else x
+            if op1 is None:
+                return e.tensor_scalar(ap(out), x, val(s1), None, op0)
+            return e.tensor_scalar(ap(out), x, val(s1), val(s2), op0, op1)
+        issue("v", fn, [a] + [s for s in (s1, s2, off) if isinstance(s, tuple)], [out])
+
+    def copy(q, out, a, off=None, scale=None, bias=None):
+        def fn(e):
+            x = ap(a)
+            x = x.indirect(ap(off)) if off else x
+            if q == "v":
+                return e.tensor_copy(ap(out), x)
+            if bias is not None:
+                return e.activation(ap(out), x, AF.Identity, bias=val(bias), scale=1.0 if scale is None else scale)
+            return e.activation(ap(out), x, AF.Copy) if scale is None else e.activation(ap(out), x, AF.Copy, scale=scale)
+        issue(q, fn, [a] + [r for r in (off, bias) if isinstance(r, tuple)], [out])
+
+    def turn(out, a):
+        issue("v", lambda e: e.transpose(ap(out), ap(a)), [a], [out])
+
+    def quant(name, c0, c1, tile, t0):
+        q, s, t = R(name, c0, c1), R(name + "s", c0, c1), R(tile, t0, t0 + 4 * (c1 - c0))
+        issue("v", lambda e: e.quantize_mx(ap(q), ap(s), ap(t)), [t], [q, s])
+
+    def mm(bank, n, lhs, l0, rhs, c0, start=True, stop=True):
+        out = R("ps%d" % bank, 0, n)
+        a, sa, b, sb = R(lhs, l0, l0 + 128), R(lhs + "s", l0, l0 + 128), R(rhs, c0, c0 + n), R(rhs + "s", c0, c0 + n)
+        issue("t", lambda e: e.matmul_mx(ap(out), ap(a), ap(sa), ap(b), ap(sb), start, stop), [a, sa, b, sb], [out])
+
+    def iota(r, pattern, base, mult, flag=False):
+        if flag:
+            issue("g", lambda e: e.iota(ap(r), pattern, base, mult, allow_small_or_imprecise_dtypes=True), [], [r])
+        else:
+            issue("g", lambda e: e.iota(ap(r), pattern, base, mult), [], [r])
+
+    def select(out, in_, pattern, base, mult):
+        issue("g", lambda e: e.affine_select(ap(out), ap(in_), pattern, OP.is_equal, 0.0, base, mult), [in_], [out])
+
+    full = R("tr", 0, 8 * ROW)
+    chunks = [(0, HALF), (HALF, C)]
+
+    dma("y", "mt", R("mti", 0, 24), None, T.mt[:, :])
+    for k, (a, b) in enumerate(chunks):
+        dma("y", "x%d" % k, R("xt", 4 * a, 4 * b), None, T.x[:, 4 * a:4 * b])
+    dma("s", "la", R("offi", 0, 24, 1, 0, 16), None, T.la[:, :])
+    dma("s", "la", R("offi", 0, 24, 1, 112, 128), None, T.lb[:, :])
+    dma("s", "la", R("offi", 0, 24, 1, 16, 112), None, T.mt[16:112, :])
+    dma("s", "u", R("ut", 0, 512), None, T.u[:, :])
+
+    iota(R("ip", 0, 1), [[0, 1]], 0, 1)
+    iota(R("ik", 0, 2), [[16, 2]], 0, 0)
+    iota(R("idf", 0, 400), [[1, 400]], -HALF, 0, True)
+    memset(R("fl", 0, ROW), 0.0)
+    for k in range(1, 4):
+        dma("y", "fl", R("fl", ROW * k, ROW * (k + 1)), R("fl", 0, ROW))
+    memset(R("onem", 0, 512), -1.0)
+    memset(R("onem", 0, 512, 64), 1.0)
+    memset(R("onem", 28, 512, 64), 1.0)
+    ts(P("i15"), P("ip"), 15, None, OP.bitwise_and)
+    ts(P("b16"), P("ip"), 16, None, OP.bitwise_and)
+    ts(P("ph"), P("ip"), 4, None, OP.logical_shift_right)
+    copy("v", P("p15"), P("i15"))
+    ts(P("cb"), P("b16"), -1.0, 208.0, OP.mult, OP.add)
+    ts(P("cm"), P("b16"), -16.0, None, OP.add)
+    ts(P("cn"), P("b16"), -1.0, 16.0, OP.mult, OP.add)
+    ts(P("c32"), P("b16"), -1.0, 32.0, OP.mult, OP.add)
+    memset(R("delta", 0, 400), 0.0)
+    memset(R("ones", 0, 512), 1.0)
+    ts(P("t1"), P("ph"), 0.0, 8.0, OP.is_gt, OP.mult)
+    ts(P("t2"), P("ph"), 7.0, 8.0, OP.is_lt, OP.mult)
+    ts(P("t3"), P("ph"), 6.0, 7.0, OP.is_equal, OP.mult)
+    ts(P("bs1"), P("ph"), float(ROW), P("c32"), OP.mult, OP.add)
+    ts(P("bs2"), P("ph"), -float(ROW), 7.0 * ROW, OP.mult, OP.add)
+    ts(R("k2", 0, 2), R("ik", 0, 2), P("p15"), 23.0, OP.add, OP.min)
+    copy("s", R("idc", 0, C), R("idf", 0, C))
+    copy("s", R("base", 0, 400), R("idf", 0, 400), bias=P("cm"))
+    memset(R("mi", 0, 26), 0)
+    memset(R("new", 0, 16), 0.0)
+    memset(R("f1", 0, 16), 0.0)
+    select(R("c0", 0, 512), R("onem", 0, 512), [[0, 8], [-16, 16], [1000, 4]], 0, 1)
+    select(R("ce", 0, 512), R("c0", 0, 512), [[0, 4], [1, 2], [0, 64]], 0, 0)
+    select(R("cd", 0, 512), R("c0", 0, 512), [[0, 4], [1, 2], [0, 64]], -1, 0)
+    for b in range(4):
+        select(R("e%d" % b, 0, 512), R("ones", 0, 512), [[1, 512]], -b, -4)
+
+    copy("v", R("mt16", 0, 24), R("mti", 0, 24))
+    copy("v", R("offa", 0, 24), R("offi", 0, 24))
+    copy("s", R("r0", 0, C), R("idf", 0, C), R("offa", 0, 24))
+    tt(R("wf", 0, C), R("idf", 0, C), R("idc", 0, C), OP.is_gt, R("mt16", 0, 24))
+    copy("s", R("wsg", 0, C), R("wf", 0, C), scale=2.0, bias=-1.0)
+    for s, p in ((0, 0), (7, 112)):
+        for h in (0, 16):
+            dma("y", "bs", R("base", 16 - h, 16 - h + C, 1, h + s, 128, 32), R("r0", 0, C, 1, p, p + 4))
+    quant("uq", 0, 128, "ut", 0)
+
+    def scores(k):
+        a, b = chunks[k]
+        mm(k, HALF, "uq", 0, "xq", a)
+
+    copy("v", R("r0c", 0, C), R("r0", 0, C))
+    for k, (a, b) in enumerate(chunks):
+        quant("xq", a, b, "xt", 4 * a)
+        scores(k)
+        if k == 0:
+            tt(R("dl8", 0, C), R("r0", 0, C), R("r0c", 0, C), OP.subtract, R("mt16", 0, 24))
+    for h in range(8):
+        o = 16 * (1 - h % 2)
+        dma("ys"[h % 2], "dl", R("delta", o, o + C, 1, 16 * h, 16 * h + 8), R("dl8", 0, C, 1, 0, 128, 16))
+    dma("y", "wc", ("wq", (0, 512, 1), (0, 128, 1), True), None, T.wc[:, :])
+    dma("y", "ws", R("wqs", 0, 512), None, T.ws[:, :])
+    for h in range(8):
+        o = 1 - h % 2
+        m = 0 if h < 4 else 112
+        dma("y", "mi", R("mi", o, o + 24, 1, 16 * h, 16 * h + 16), None, T.mt[m:m + 16, :])
+    dma("y", "v", R("vt", 0, 512), None, T.v[:, :])
+
+    def gather(out, win, off, m=NV):
+        copy("v", R(out, 16, 16 + 16 * m), R(win, 16, ROW), R(off, 0, m))
+        copy("s", R(out, 16 + 16 * m, ROW), R(win, 16, ROW), R(off, m, 25))
+
+    def place(off, k, slot):
+        ts(R(off, 0, 25), R("tr", ROW * k + 16 + slot, ROW * (k + 1), 16), P("cb"), None, OP.add)
+
+    for rnd, step in enumerate(STEP):
+        mate = T.cores[rank ^ step]
+        last = rnd == len(STEP) - 1
+        for k, (a, b) in enumerate(chunks):
+            tt(R("sw", a, b), R("ps%d" % k, 0, HALF), R("wsg", a, b), OP.mult)
+            copy("s", R("ns", a, b), R("sw", a, b), scale=-1.0)
+        if rnd == 0:
+            quant("ceq", 0, 128, "ce", 0)
+            quant("cdq", 0, 128, "cd", 0)
+        def flags(k):
+            a, b = ZCH[k]
+            tt(R("fl", 4 * (a + 16), 4 * (b + 16), 4), R("sw", 0, C), R("ns", a, b), OP.is_lt, R("mt16", a // 16, b // 16))
+
+        def spread(k):
+            a, b = ((0, 144), (144, 272), (272, ROW))[k]
+            quant("fq", a, b, "fl", 4 * a)
+            a, b = NCH[k]
+            mm(2 + k, b - a, "ceq", 0, "fq", a, True, False)
+            mm(2 + k, b - a, "cdq", 0, "fq", a + 16, False, True)
+
+        flags(0)
+        flags(1)
+        spread(0)
+        flags(2)
+        spread(1)
+        spread(2)
+        for t in range(4):
+            copy("s", R("xp%d" % t, 0, C), R("xt", t, 4 * C, 4))
+        if rnd == 0:
+            tt(P("t3"), P("t3"), P("c32"), OP.add)
+            tt(P("t2"), P("t2"), P("c32"), OP.add)
+            tt(P("bs1"), P("bs1"), P("t1"), OP.add)
+            tt(P("bs2"), P("bs2"), P("t2"), OP.add)
+            ts(R("sel", 0, 2), R("k2", 0, 2), 16.0, P("bs1"), OP.mult, OP.add)
+            ts(R("sel", 2, 4), R("k2", 0, 2), 16.0, P("bs2"), OP.mult, OP.add)
+            ts(R("sel", 4, 6), R("k2", 0, 2), 16.0, P("t3"), OP.mult, OP.add)
+            for k in range(2, 8):
+                copy("s", R("f%d" % k, 0, 16), R("new", 0, 16))
+
+        def change(k):
+            a, b = NCH[k]
+            tt(R("tm", a, b), R("ps%d" % (2 + k), 0, b - a), R("delta", a, b), OP.mult)
+
+        def renew(k):
+            a, b = NCH[k]
+            tt(R("new", 16 + a, 16 + b), R("tm", a, b), R("base", a, b), OP.add)
+
+        change(0)
+        change(1)
+        renew(0)
+        change(2)
+        renew(1)
+        renew(2)
+        turn(R("tr", 0, 256), R("new", 0, 256))
+        turn(R("tr", 256, ROW), R("new", 256, ROW))
+        place("ob", 0, 7)
+        gather("f1", "new", "ob")
+        place("oa", 0, 0)
+        turn(R("tr", ROW, ROW + HALF), R("f1", 0, HALF))
+        turn(R("tr", ROW + HALF, 2 * ROW), R("f1", HALF, ROW))
+        gather("f0", "new", "oa", 8)
+        if rnd == 0:
+            ts(R("lf", 64, 96), R("tr", 0, ROW), float(HALF), None, OP.add, None, R("sel", 4, 6))
+            remote(R("le", 0, 24), R("lf", 64, 88), mate, "are", "loe", topo, core)
+            arrives(R("le", 0, 24), "are", len(topo.engines(mate, core)))
+        place("ok1", 1, 1)
+        for k in range(1, 7):
+            gather("pa", "f%d" % (k - 1), "ok%d" % k)
+            gather("f%d" % (k + 1), "pa", "ok%d" % k)
+            o = ROW * (k + 1)
+            turn(R("tr", o, o + HALF), R("f%d" % (k + 1), 0, HALF))
+            turn(R("tr", o + HALF, o + ROW), R("f%d" % (k + 1), HALF, ROW))
+            if k < 6:
+                place("ok%d" % (k + 1), k + 1, k + 1)
+        if last:
+            dma("y", "st", R("lb16", 0, C, 1, 0, 1), R("new", 32, ROW, 1, 0, 1))
+            for k in range(1, 8):
+                dma("y", "st", R("lb16", 0, C, 1, k, k + 1), R("f%d" % k, 32, ROW, 1, 8, 9))
+        else:
+            for s in (0, 7):
+                dma("y", "nb%d" % rnd, R("base", 0, 400, 1, s, 128, 16), R("new", 16, ROW, 1, s, 128, 16))
+        ts(R("lf", 0, 64), full, float(HALF), None, OP.add, None, R("sel", 0, 4))
+        remote(R("lr%d" % rnd, 0, 24), R("lf", 32, 56), mate, "ar%dl" % rnd, "lo%dl" % rnd, topo, core)
+        n = len(topo.engines(mate, core))
+        arrives(R("lr%d" % rnd, 0, 24), "ar%dl" % rnd, n)
+        def layer(k):
+            a, b = ZCH[k]
+            for i in (0, 2, 1, 3):
+                mm((4, 0)[k % 2] + i, b - a, "wq", 128 * i, "zq", a)
+
+        def result(k, i):
+            a, b = ZCH[k]
+            src, dst = R("ps%d" % ((4, 0)[k % 2] + i), 0, b - a), R("hp%d" % i, a, b)
+            if i < 2:
+                ts(dst, src, 0.03125, None, OP.mult)
+            else:
+                copy("s", dst, src, scale=0.03125)
+
+        def parts(k, t):
+            a, b = SCH[k]
+            copy("vvss"[t], R("hg", 4 * a + t, 4 * b, 4), R("hp%d" % t, 0, C), R("lm" if rnd == 0 else "lr%d" % rnd, a // 16, b // 16))
+
+        def zed(k, t):
+            a, b = ZCH[k]
+            copy("vvss"[t], R("zt", 4 * a + t, 4 * b, 4), R("xp%d" % t, 0, C), R("lf", a // 16, b // 16))
+
+        for t in range(4):
+            zed(0, t)
+        for k, (a, b) in enumerate(ZCH):
+            if k + 1 < len(ZCH):
+                zed(k + 1, 0)
+                zed(k + 1, 2)
+                zed(k + 1, 3)
+            quant("zq", a, b, "zt", 4 * a)
+            if k + 1 < len(ZCH):
+                zed(k + 1, 1)
+            if k < 2:
+                layer(k)
+        for k in range(len(ZCH) - 1):
+            for i in (0, 2, 1, 3):
+                result(k, i)
+            if k == 0:
+                for j in range(2, len(ZCH)):
+                    layer(j)
+        if rnd == 0:
+            copy("v", R("lm", 0, 24, 1, 96, 128), R("le", 0, 24, 1, 96, 128))
+            copy("v", R("lm", 0, 24, 1, 0, 96), R("lr0", 0, 24, 1, 0, 96))
+        for i in (0, 2, 1, 3):
+            result(len(ZCH) - 1, i)
+        for i in (0, 2, 1, 3):
+            parts(0, i)
+        for k, (a, b) in enumerate(SCH):
+            if k:
+                for t in range(4):
+                    parts(k, t)
+            quant("hq", a, b, "hg", 4 * a)
+            remote(B("hr%d" % rnd, a, b), B("hq", a, b), mate, "ar%dc%d" % (rnd, k), "lo%dc%d" % (rnd, k), topo, core)
+            remote(R("hr%ds" % rnd, a, b), R("hqs", a, b), mate, "ar%ds%d" % (rnd, k), "lo%ds%d" % (rnd, k), topo, core)
+        for k, (a, b) in enumerate(SCH):
+            arrives(R("hr%d" % rnd, a, b), "ar%dc%d" % (rnd, k), n)
+            arrives(R("hr%ds" % rnd, a, b), "ar%ds%d" % (rnd, k), n)
+        if rnd == 0:
+            for b in range(4):
+                quant("e%dq" % b, 0, 128, "e%d" % b, 0)
+            ts(R("ml", 0, 25), R("mi", 0, 25), P("cn"), None, OP.add)
+        if rnd == 1:
+            quant("vq", 0, 128, "vt", 0)
+        if not last:
+            copy("s", R("newc", 0, 400), R("new", 16, ROW))
+            tt(R("dab", 0, 400), R("new", 16, ROW), R("newc", 0, 400), OP.subtract, R("ml", 0, 25))
+            for s, p in ((0, 0), (7, 64)):
+                for h in (0, 64):
+                    dma("y", "nd%d" % rnd, R("delta", 0, 400, 1, h + s, h + 64, 16), R("dab", 0, 400, 1, p + s, p + 64, 16))
+        else:
+            copy("s", R("l32", 0, C, 1, 0, 8), R("lb16", 0, C, 1, 0, 8), bias=float(HALF))
+            dma("y", "out", None, R("l32", 0, C, 1, 0, 8), None, T.ll[:, :])
+        for k, (a, b) in enumerate(chunks):
+            for i in range(4):
+                mm((4, 0)[k] + i, HALF, "e%dq" % i, 0, "hr%d" % rnd, a)
+        def grow(k, i):
+            a, b = chunks[k]
+            x = R("xt", 4 * a + i, 4 * b, 4)
+            tt(x, R("ps%d" % ((4, 0)[k] + i), 0, HALF), x, OP.add)
+
+        for i in range(4):
+            grow(0, i)
+        grow(1, 0)
+        for k, (a, b) in enumerate(chunks):
+            if k:
+                for i in range(1, 4):
+                    grow(1, i)
+            quant("xq", a, b, "xt", 4 * a)
+            if not last:
+                continue
+            dma("y", "out", None, B("xq", a, b), None, T.oc[:, 4 * a:4 * b])
+            for i in range(4):
+                dma("y", "out", None, R("xqs", a, b, 1, 32 * i, 32 * i + 4), None, T.osc[4 * i:4 * i + 4, a:b])
+            mm(4 + k, HALF, "vq", 0, "xq", a)
+            copy("s", R("ysb", a, b), R("ps%d" % (4 + k), 0, HALF))
+            dma("s", "out", None, R("ysb", a, b), None, T.y[:, a:b])
+        if not last:
+            for k in range(2):
+                scores(k)
+    finish()

@@ -2,12 +2,17 @@ from concourse.mybir import dt, AluOpType as OP, ActivationFunctionType as AF
 
 C = 384
 HALF = C // 2
-SCH = [(0, HALF), (HALF, C)]
-ZCH = [(0, 128), (128, 256), (256, 384)]
-NCH = [(0, 128), (128, 256), (256, 400)]
 STEP = [1, 2, 4]
 ROW = 416
-NV = 12
+THIRDS = [(0, 128), (128, 256), (256, 384)]
+NCH = [(0, 128), (128, 256), (256, 400)]
+PLAIN = 8
+CFG = {"sch": [(0, HALF), (HALF, C)], "na": 12, "nb": 6, "n0": 8,
+       "p4": "z00v z02s z01v z03s z12s q0 z10v l00 l02 l01 l03 z13s z11v z22s z20v q1 z23s z21v l10 l12 r00s q2 l11 r02s r01v r03v r10s l20 l22 r12s l13 l21 l23 "
+             "r11v m r20v r22s p00v p02s r13s r21v r23s p01v p03s p10v h0 p12s p11v p13s h1",
+       "p5": "u0 u1 g00 g01 g02 g03 g10 x0 g11 g12 g13 n0 x1 w0 w1 n1"}
+
+ONE = ["cb", "cn", "cm", "c32", "phf", "gp", "gm", "gn", "ng", "zb", "bs1", "bs2", "bs3", "t1", "t2"]
 
 SCRATCH = {}
 SEMAPHORES = ["cv", "cs", "ct", "cg", "are", "loe"]
@@ -17,25 +22,26 @@ def _declare():
     def sb(name, cols, dtype):
         SCRATCH[name] = ("sbuf", [128, cols], dtype)
     bf, f32, i32, u16, co, u8 = "bfloat16", "float32", "int32", "uint16", "float8_e4m3fn_x4", "uint8"
-    for n, c in (("xt", 4 * C), ("ut", 512), ("vt", 512), ("zt", 4 * C), ("hg", 4 * C), ("fl", 4 * ROW), ("ones", 512), ("onem", 512), ("c0", 512),
-                 ("ce", 512), ("cd", 512), ("e0", 512), ("e1", 512), ("e2", 512), ("e3", 512), ("r0", C), ("r0c", C), ("newc", 400), ("idc", C), ("base", 400),
-                 ("new", ROW), ("pa", ROW), ("tr", 8 * ROW), ("lb16", C)):
+    for n, c in (("xt", 4 * C), ("ut", 512), ("vt", 512), ("zt", 4 * C), ("hg", 4 * C), ("fl", 4 * ROW), ("ones", 512), ("cc", 576), ("sr", 128),
+                 ("e0", 512), ("e1", 512), ("e2", 512), ("e3", 512), ("base", 400), ("tb", 896), ("w1", C), ("w2", C),
+                 ("new", ROW), ("na", ROW), ("fb", ROW), ("tr", 8 * ROW + 32), ("lb16", C)):
         sb(n, c, bf)
     for b in range(4):
         sb("xp%d" % b, C, bf)
         sb("hp%d" % b, C, bf)
-    for k in range(8):
+    for k in range(1, 8):
         sb("f%d" % k, ROW, bf)
-    for n, c in (("idf", 400), ("wsg", C), ("wf", C), ("dl8", C), ("delta", 400), ("tm", 400), ("dab", 400), ("sw", C), ("ns", C), ("ysb", C), ("l32", C),
-                 ("cb", 1), ("cn", 1), ("cm", 1), ("p15", 1), ("c32", 1), ("bs1", 1), ("t1", 1), ("t2", 1), ("t3", 1), ("bs2", 1), ("k2", 2)):
+    for n, c in (("vi", 512), ("sw", C), ("ns", C), ("ysb", C), ("l32", C), ("d0", 64), ("d1", 64), ("cr", 64), ("ct", 64), ("dw", 24),
+                 ("k2", 2), ("one", len(ONE))):
         sb(n, c, f32)
-    for n, c in (("mti", 24), ("offi", 24), ("ip", 1), ("b16", 1), ("i15", 1), ("ph", 1), ("ik", 2), ("mi", 26)):
+    for n, c in (("mti", 24), ("iw", 24), ("b16", 1), ("i15", 1), ("ph", 1), ("mi", 26), ("zi", 512), ("zp", 512)):
         sb(n, c, i32)
-    for n, c in (("mt16", 24), ("offa", 24), ("sel", 6), ("ml", 26), ("oa", 26), ("ob", 26), ("lf", 96), ("le", 24), ("lm", 24)):
+    for n, c in (("mt16", 24), ("o1", 24), ("o2", 24), ("ou", 8), ("sel", 6), ("oab", 26), ("opi", 26), ("lz", 32), ("ls", 32), ("l0", 32), ("le", 24), ("lm", 24)):
         sb(n, c, u16)
-    for k in range(1, 7):
-        sb("ok%d" % k, 26, u16)
-    for n, c in (("xq", C), ("uq", 128), ("vq", 128), ("zq", C), ("hq", C), ("fq", ROW), ("wq", 512), ("ceq", 128), ("cdq", 128),
+    for k in range(7):
+        sb("oa%d" % k, 26, u16)
+        sb("ob%d" % k, 26, u16)
+    for n, c in (("xq", C), ("u0q", 128), ("uq", 128), ("vq", 128), ("zq", C), ("hq", C), ("fq", ROW), ("wq", 512), ("cq", 144),
                  ("e0q", 128), ("e1q", 128), ("e2q", 128), ("e3q", 128)):
         sb(n, c, co)
         sb(n + "s", c, u8)
@@ -46,14 +52,11 @@ def _declare():
     for k in range(8):
         SCRATCH["ps%d" % k] = ("psum", [128, 512], f32)
     for r in range(3):
-        for n in ("l", "c0", "s0", "c1", "s1"):
+        for n in ("l", "c0", "s0", "c1", "s1", "c2", "s2"):
             SEMAPHORES.append("ar%d%s" % (r, n))
             SEMAPHORES.append("lo%d%s" % (r, n))
-    for n in ("x0", "x1", "mt", "u", "v", "la", "wc", "ws", "mi", "fl", "bs", "dl", "st", "out"):
+    for n in ("x0", "x1", "x2", "mt", "u", "v", "wc", "ws", "mi", "st", "out"):
         SEMAPHORES.append("d_" + n)
-    for r in range(2):
-        SEMAPHORES.append("d_nb%d" % r)
-        SEMAPHORES.append("d_nd%d" % r)
 
 
 _declare()
@@ -164,8 +167,10 @@ def rank_program(g, core, T, topo):
     def B(name, c0, c1):
         return (name, (c0, c1, 1), (0, 128, 1), True)
 
-    def P(name, p0=0, p1=128):
-        return R(name, 0, 1, 1, p0, p1)
+    def P(name, p0=0, p1=128, c=0):
+        if name in ONE:
+            name, c = "one", ONE.index(name)
+        return R(name, c, c + 1, 1, p0, p1)
 
     def dma(q, sem, out, in_, ext_in=None, ext_out=None):
         issue(q, lambda e: e.dma_start(ext_out if ext_out is not None else ap(out), ext_in if ext_in is not None else ap(in_)),
@@ -199,9 +204,9 @@ def rank_program(g, core, T, topo):
             if q == "v":
                 return e.tensor_copy(ap(out), x)
             if bias is not None:
-                return e.activation(ap(out), x, AF.Identity, bias=val(bias), scale=1.0 if scale is None else scale)
-            return e.activation(ap(out), x, AF.Copy) if scale is None else e.activation(ap(out), x, AF.Copy, scale=scale)
-        issue(q, fn, [a] + [r for r in (off, bias) if isinstance(r, tuple)], [out])
+                return e.activation(ap(out), x, AF.Identity, bias=val(bias), scale=1.0 if scale is None else val(scale))
+            return e.activation(ap(out), x, AF.Copy) if scale is None else e.activation(ap(out), x, AF.Copy, scale=val(scale))
+        issue(q, fn, [a] + [r for r in (off, bias, scale) if isinstance(r, tuple)], [out])
 
     def turn(out, a):
         issue("v", lambda e: e.transpose(ap(out), ap(a)), [a], [out])
@@ -224,272 +229,316 @@ def rank_program(g, core, T, topo):
     def select(out, in_, pattern, base, mult):
         issue("g", lambda e: e.affine_select(ap(out), ap(in_), pattern, OP.is_equal, 0.0, base, mult), [in_], [out])
 
-    full = R("tr", 0, 8 * ROW)
-    chunks = [(0, HALF), (HALF, C)]
+    sch = CFG["sch"]
+    pw, zs = P("ct"), P("ct", c=32)
 
-    dma("y", "mt", R("mti", 0, 24), None, T.mt[:, :])
-    for k, (a, b) in enumerate(chunks):
+    dma("s", "mt", R("mti", 0, 24), None, T.mt[:, :])
+    for k, (a, b) in enumerate(sch):
         dma("y", "x%d" % k, R("xt", 4 * a, 4 * b), None, T.x[:, 4 * a:4 * b])
-    dma("s", "la", R("offi", 0, 24, 1, 0, 16), None, T.la[:, :])
-    dma("s", "la", R("offi", 0, 24, 1, 112, 128), None, T.lb[:, :])
-    dma("s", "la", R("offi", 0, 24, 1, 16, 112), None, T.mt[16:112, :])
     dma("s", "u", R("ut", 0, 512), None, T.u[:, :])
 
-    iota(R("ip", 0, 1), [[0, 1]], 0, 1)
-    iota(R("ik", 0, 2), [[16, 2]], 0, 0)
-    iota(R("idf", 0, 400), [[1, 400]], -HALF, 0, True)
-    memset(R("fl", 0, ROW), 0.0)
-    for k in range(1, 4):
-        dma("y", "fl", R("fl", ROW * k, ROW * (k + 1)), R("fl", 0, ROW))
-    memset(R("onem", 0, 512), -1.0)
-    memset(R("onem", 0, 512, 64), 1.0)
-    memset(R("onem", 28, 512, 64), 1.0)
-    ts(P("i15"), P("ip"), 15, None, OP.bitwise_and)
-    ts(P("b16"), P("ip"), 16, None, OP.bitwise_and)
-    ts(P("ph"), P("ip"), 4, None, OP.logical_shift_right)
-    copy("v", P("p15"), P("i15"))
-    ts(P("cb"), P("b16"), -1.0, 208.0, OP.mult, OP.add)
-    ts(P("cm"), P("b16"), -16.0, None, OP.add)
-    ts(P("cn"), P("b16"), -1.0, 16.0, OP.mult, OP.add)
-    ts(P("c32"), P("b16"), -1.0, 32.0, OP.mult, OP.add)
-    memset(R("delta", 0, 400), 0.0)
-    memset(R("ones", 0, 512), 1.0)
-    ts(P("t1"), P("ph"), 0.0, 8.0, OP.is_gt, OP.mult)
-    ts(P("t2"), P("ph"), 7.0, 8.0, OP.is_lt, OP.mult)
-    ts(P("t3"), P("ph"), 6.0, 7.0, OP.is_equal, OP.mult)
-    ts(P("bs1"), P("ph"), float(ROW), P("c32"), OP.mult, OP.add)
-    ts(P("bs2"), P("ph"), -float(ROW), 7.0 * ROW, OP.mult, OP.add)
-    ts(R("k2", 0, 2), R("ik", 0, 2), P("p15"), 23.0, OP.add, OP.min)
-    copy("s", R("idc", 0, C), R("idf", 0, C))
-    copy("s", R("base", 0, 400), R("idf", 0, 400), bias=P("cm"))
-    memset(R("mi", 0, 26), 0)
-    memset(R("new", 0, 16), 0.0)
-    memset(R("f1", 0, 16), 0.0)
-    select(R("c0", 0, 512), R("onem", 0, 512), [[0, 8], [-16, 16], [1000, 4]], 0, 1)
-    select(R("ce", 0, 512), R("c0", 0, 512), [[0, 4], [1, 2], [0, 64]], 0, 0)
-    select(R("cd", 0, 512), R("c0", 0, 512), [[0, 4], [1, 2], [0, 64]], -1, 0)
+    iota(R("vi", 0, 512), [[1, 512]], 512, 0, True)
+    iota(R("iw", 0, 24), [[16, 24]], 0, 1)
+    for h in range(2):
+        iota(R("sr", 64 * h, 64 * h + 64), [[0, 2], [64, 2], [2, 16]], -h, 0, True)
+    iota(R("ones", 0, 512), [[0, 512]], 1, 0, True)
     for b in range(4):
         select(R("e%d" % b, 0, 512), R("ones", 0, 512), [[1, 512]], -b, -4)
-
-    copy("v", R("mt16", 0, 24), R("mti", 0, 24))
-    copy("v", R("offa", 0, 24), R("offi", 0, 24))
-    copy("s", R("r0", 0, C), R("idf", 0, C), R("offa", 0, 24))
-    tt(R("wf", 0, C), R("idf", 0, C), R("idc", 0, C), OP.is_gt, R("mt16", 0, 24))
-    copy("s", R("wsg", 0, C), R("wf", 0, C), scale=2.0, bias=-1.0)
-    for s, p in ((0, 0), (7, 112)):
-        for h in (0, 16):
-            dma("y", "bs", R("base", 16 - h, 16 - h + C, 1, h + s, 128, 32), R("r0", 0, C, 1, p, p + 4))
-    quant("uq", 0, 128, "ut", 0)
-
-    def scores(k):
-        a, b = chunks[k]
-        mm(k, HALF, "uq", 0, "xq", a)
-
-    copy("v", R("r0c", 0, C), R("r0", 0, C))
-    for k, (a, b) in enumerate(chunks):
-        quant("xq", a, b, "xt", 4 * a)
-        scores(k)
-        if k == 0:
-            tt(R("dl8", 0, C), R("r0", 0, C), R("r0c", 0, C), OP.subtract, R("mt16", 0, 24))
-    for h in range(8):
-        o = 16 * (1 - h % 2)
-        dma("ys"[h % 2], "dl", R("delta", o, o + C, 1, 16 * h, 16 * h + 8), R("dl8", 0, C, 1, 0, 128, 16))
-    dma("y", "wc", ("wq", (0, 512, 1), (0, 128, 1), True), None, T.wc[:, :])
-    dma("y", "ws", R("wqs", 0, 512), None, T.ws[:, :])
+    memset(R("mi", 0, 26), 0)
     for h in range(8):
         o = 1 - h % 2
-        m = 0 if h < 4 else 112
-        dma("y", "mi", R("mi", o, o + 24, 1, 16 * h, 16 * h + 16), None, T.mt[m:m + 16, :])
+        dma("y", "mi", R("mi", o, o + 24, 1, 16 * h, 16 * h + 16), None, (T.la, T.lb)[h // 4][:, :])
+    dma("y", "wc", ("wq", (0, 512, 1), (0, 128, 1), True), None, T.wc[:, :])
+    dma("y", "ws", R("wqs", 0, 512), None, T.ws[:, :])
     dma("y", "v", R("vt", 0, 512), None, T.v[:, :])
+    memset(R("d0", 0, 32), 2.0)
+    memset(R("d0", 32, 64), 0.5)
+    memset(R("d1", 0, 64), 0.0)
+    memset(R("d0", 16, 48, 16), 2.0 ** -15)
+    memset(R("d0", 48, 49), 2.0 ** 15)
+    memset(R("fl", 0, ROW), 0.0)
+    issue("v", lambda e: e.tensor_tensor_scan(ap(R("cr", 0, 64)), ap(R("d0", 0, 64)), ap(R("d1", 0, 64)), 0.5, OP.mult, OP.add),
+          [R("d0", 0, 64), R("d1", 0, 64)], [R("cr", 0, 64)])
+    memset(R("cc", 0, 288), 0.0)
+    memset(R("cr", 9, 32, 16), -512.0)
+    memset(R("cc", 288, 576), 0.0)
+    turn(R("ct", 0, 64), R("cr", 0, 64))
+    for k in range(1, 4):
+        copy("s", R("fl", ROW * k, ROW * (k + 1)), R("fl", 0, ROW))
+    memset(R("new", 0, 16), 0.0)
+    memset(R("f1", 0, 16), 0.0)
+    ts(P("zb"), zs, 0.5, -0.5, OP.mult, OP.add)
+    ts(P("i15"), P("iw"), 15, None, OP.bitwise_and)
+    ts(P("ph"), P("iw"), 4, None, OP.logical_shift_right)
+    ts(R("zi", 0, 512), R("vi", 0, 512), zs, P("zb"), OP.mult, OP.add)
+    ts(P("ng"), P("i15"), 9.0, -1.0, OP.is_lt, OP.mult)
+    ts(P("gp"), P("ph"), 16.0, 512.0, OP.mult, OP.add)
+    ts(R("zp", 0, 512), R("zi", 0, 512), 1, None, OP.bitwise_and)
+    ts(P("gm"), P("ph"), -16.0, 512.0, OP.mult, OP.add)
+    tt(R("dw", 0, 24), R("mti", 0, 24), R("iw", 0, 24), OP.subtract)
+    copy("v", R("tb", 0, 512), R("zp", 0, 512))
+    ts(R("o1", 0, 24), R("dw", 0, 24), -1.0, P("gm"), OP.mult, OP.add)
+    ts(R("o2", 0, 24), R("dw", 0, 24), P("gp"), None, OP.add)
+    copy("s", R("tb", 512, 896), R("tb", 0, C), scale=P("ng"))
+    copy("s", R("w1", 0, C), R("tb", 0, 896), R("o1", 0, 24))
+    ts(R("ou", 0, 8), R("vi", 0, 128, 16), -512.0, None, OP.add)
+    quant("u0q", 0, 128, "ut", 0)
+    issue("v", lambda e: e.tensor_copy(T.uq[:, 0:128].bitcast(dt.uint32), T.u0q[:, 0:128].bitcast(dt.uint32).indirect(T.ou[:, 0:8])),
+          [R("u0q", 0, 128), R("ou", 0, 8)], [R("uq", 0, 128)])
+    copy("s", R("uqs", 0, 128), R("u0qs", 0, 128), R("ou", 0, 8))
 
-    def gather(out, win, off, m=NV):
-        copy("v", R(out, 16, 16 + 16 * m), R(win, 16, ROW), R(off, 0, m))
-        copy("s", R(out, 16 + 16 * m, ROW), R(win, 16, ROW), R(off, m, 25))
+    def bank(k, i):
+        return 4 * ((k + 1) % 2) + i
 
-    def place(off, k, slot):
-        ts(R(off, 0, 25), R("tr", ROW * k + 16 + slot, ROW * (k + 1), 16), P("cb"), None, OP.add)
+    def scores(k):
+        a, b = sch[k]
+        quant("xq", a, b, "xt", 4 * a)
+        mm(bank(k, 0), b - a, "uq", 0, "xq", a)
+
+    def minus(k):
+        a, b = sch[k]
+        tt(R("ns", a, b), R("ps%d" % bank(k, 0), 0, b - a), R("w2", a, b), OP.mult)
+
+    def plus(k):
+        a, b = sch[k]
+        tt(R("sw", a, b), R("ps%d" % bank(k, 0), 0, b - a), R("w1", a, b), OP.mult)
+
+    def signed(k):
+        plus(k)
+        minus(k)
+
+    scores(0)
+    copy("v", R("w2", 0, C), R("tb", 0, 896), R("o2", 0, 24))
+    scores(1)
+    copy("v", R("mt16", 0, 24), R("mti", 0, 24))
+    ts(P("b16"), P("iw"), 16, None, OP.bitwise_and)
+    copy("v", P("phf"), P("ph"))
+    memset(R("sr", 64, 128, 32), 7.0)
+    for k in range(len(sch)):
+        if k > 1:
+            scores(k)
+        if k == len(sch) - 1:
+            ts(P("cm"), P("b16"), -16.0 - 512 - HALF, None, OP.add)
+            ts(R("cc", 64, 576, 4), R("sr", 0, 128), P("phf"), pw, OP.is_equal, OP.mult)
+            copy("s", R("base", 0, 400), R("vi", 0, 400), bias=P("cm"))
+        signed(k)
+
+    def half(k):
+        return (64 * (k % 2), 64 * (k % 2) + 64)
+
+    def gather(q, out, win, off, m):
+        if q == "v":
+            copy("v", R(out, 16, 16 + 16 * m), R(win, 16, ROW), R(off, 0, m))
+        else:
+            copy("s", R(out, 16 + 16 * m, ROW), R(win, 16, ROW), R(off, m, 25))
+
+    def both(out, win, off, m):
+        gather("v", out, win, off, m)
+        gather("s", out, win, off, m)
+
+    def place(off, k, slot, to=(0, 128), of=None):
+        of = of or to
+        ts(R(off, 0, 25, 1, *to), R("tr", ROW * k + 16 + slot, ROW * (k + 1), 16, *of), P("cb", *to), None, OP.add)
+
+    def across(k, h, shift=0):
+        o = ROW * k + 16 + PLAIN
+        copy("s", R("tr", o + shift, ROW * (k + 1), 16, *half(h + 1)), R("tr", o, ROW * (k + 1), 16, *half(h)))
+
+    def turns(k, name, cut=HALF):
+        turn(R("tr", ROW * k, ROW * k + cut), R(name, 0, cut))
+        turn(R("tr", ROW * k + cut, ROW * (k + 1)), R(name, cut, ROW))
+
+    def slot(k):
+        return (k + 1) // 2
 
     for rnd, step in enumerate(STEP):
         mate = T.cores[rank ^ step]
         last = rnd == len(STEP) - 1
-        for k, (a, b) in enumerate(chunks):
-            tt(R("sw", a, b), R("ps%d" % k, 0, HALF), R("wsg", a, b), OP.mult)
-            copy("s", R("ns", a, b), R("sw", a, b), scale=-1.0)
-        if rnd == 0:
-            quant("ceq", 0, 128, "ce", 0)
-            quant("cdq", 0, 128, "cd", 0)
+        n = len(topo.engines(mate, core))
+
         def flags(k):
-            a, b = ZCH[k]
+            a, b = THIRDS[k]
             tt(R("fl", 4 * (a + 16), 4 * (b + 16), 4), R("sw", 0, C), R("ns", a, b), OP.is_lt, R("mt16", a // 16, b // 16))
 
         def spread(k):
             a, b = ((0, 144), (144, 272), (272, ROW))[k]
             quant("fq", a, b, "fl", 4 * a)
             a, b = NCH[k]
-            mm(2 + k, b - a, "ceq", 0, "fq", a, True, False)
-            mm(2 + k, b - a, "cdq", 0, "fq", a + 16, False, True)
+            mm(1 + k, b - a, "cq", 16, "fq", a, True, False)
+            mm(1 + k, b - a, "cq", 0, "fq", a + 16, False, True)
 
+        def renew(k):
+            a, b = NCH[k]
+            tt(R("new", 16 + a, 16 + b), R("ps%d" % (1 + k), 0, b - a), R("base", a, b), OP.add)
+
+        for t in range(4):
+            copy("s", R("xp%d" % t, 0, C), R("xt", t, 4 * C, 4))
+        if rnd == 0:
+            quant("cq", 0, 144, "cc", 0)
+            ts(P("cn"), P("b16"), -1.0, 16.0, OP.mult, OP.add)
         flags(0)
         flags(1)
         spread(0)
         flags(2)
         spread(1)
-        spread(2)
-        for t in range(4):
-            copy("s", R("xp%d" % t, 0, C), R("xt", t, 4 * C, 4))
         if rnd == 0:
-            tt(P("t3"), P("t3"), P("c32"), OP.add)
-            tt(P("t2"), P("t2"), P("c32"), OP.add)
-            tt(P("bs1"), P("bs1"), P("t1"), OP.add)
-            tt(P("bs2"), P("bs2"), P("t2"), OP.add)
-            ts(R("sel", 0, 2), R("k2", 0, 2), 16.0, P("bs1"), OP.mult, OP.add)
-            ts(R("sel", 2, 4), R("k2", 0, 2), 16.0, P("bs2"), OP.mult, OP.add)
-            ts(R("sel", 4, 6), R("k2", 0, 2), 16.0, P("t3"), OP.mult, OP.add)
+            ts(R("oab", 0, 25), R("mi", 0, 25), P("cn"), None, OP.add)
+            ts(P("cb"), P("b16"), -1.0, 208.0, OP.mult, OP.add)
+        spread(2)
+        renew(0)
+        if rnd == 0:
+            ts(P("c32"), P("b16"), -1.0, 32.0 + PLAIN, OP.mult, OP.add)
+            ts(P("gn"), P("ph"), -16.0, None, OP.mult)
             for k in range(2, 8):
                 copy("s", R("f%d" % k, 0, 16), R("new", 0, 16))
-
-        def change(k):
-            a, b = NCH[k]
-            tt(R("tm", a, b), R("ps%d" % (2 + k), 0, b - a), R("delta", a, b), OP.mult)
-
-        def renew(k):
-            a, b = NCH[k]
-            tt(R("new", 16 + a, 16 + b), R("tm", a, b), R("base", a, b), OP.add)
-
-        change(0)
-        change(1)
-        renew(0)
-        change(2)
         renew(1)
+        turn(R("tr", 0, 128), R("new", 0, 128))
         renew(2)
-        turn(R("tr", 0, 256), R("new", 0, 256))
+        turn(R("tr", 128, 256), R("new", 128, 256))
         turn(R("tr", 256, ROW), R("new", 256, ROW))
-        place("ob", 0, 7)
-        gather("f1", "new", "ob")
-        place("oa", 0, 0)
-        turn(R("tr", ROW, ROW + HALF), R("f1", 0, HALF))
-        turn(R("tr", ROW + HALF, 2 * ROW), R("f1", HALF, ROW))
-        gather("f0", "new", "oa", 8)
+        gather("s", "na", "new", "oab", CFG["n0"])
+        gather("v", "na", "new", "oab", CFG["n0"])
+        place("opi", 0, 0)
         if rnd == 0:
-            ts(R("lf", 64, 96), R("tr", 0, ROW), float(HALF), None, OP.add, None, R("sel", 4, 6))
-            remote(R("le", 0, 24), R("lf", 64, 88), mate, "are", "loe", topo, core)
-            arrives(R("le", 0, 24), "are", len(topo.engines(mate, core)))
-        place("ok1", 1, 1)
+            ts(P("t1"), P("ph"), 1.0, P("c32"), OP.is_equal, OP.add)
+            ts(P("t2"), P("ph"), 7.0, P("c32"), OP.is_equal, OP.add)
+        both("f1", "na", "opi", CFG["na"])
+        if rnd == 0:
+            ts(P("bs1"), P("ph"), 1.0, float(ROW), OP.max, OP.mult)
+            ts(P("bs2"), P("ph"), 6.0, -float(ROW), OP.min, OP.mult)
+        turns(1, "f1")
+        if rnd == 0:
+            ts(R("k2", 0, 2), R("iw", 0, 2), P("gn"), 23.0, OP.add, OP.min)
+            ts(P("bs3"), P("t2"), float(ROW), None, OP.add)
+        place("ob0", 1, 1, half(0), half(1))
+        place("ob0", 1, 1, half(1), half(0))
+        place("oa1", 1, 1, half(0), half(1))
+        place("oa1", 1, 1, half(1))
+        both("fb", "f1", "ob0", CFG["na"])
+        across(1, 0, 1)
+        across(1, 1, 1)
+        place("ob1", 1, 1, half(1))
+        place("ob1", 1, 2, half(0), half(1))
         for k in range(1, 7):
-            gather("pa", "f%d" % (k - 1), "ok%d" % k)
-            gather("f%d" % (k + 1), "pa", "ok%d" % k)
-            o = ROW * (k + 1)
-            turn(R("tr", o, o + HALF), R("f%d" % (k + 1), 0, HALF))
-            turn(R("tr", o + HALF, o + ROW), R("f%d" % (k + 1), HALF, ROW))
-            if k < 6:
-                place("ok%d" % (k + 1), k + 1, k + 1)
+            name = "f%d" % (k + 1)
+            both(name, "fb", "oa%d" % k, CFG["na"])
+            if k > 1:
+                across(k, k)
+            if rnd == 0 and k == 1:
+                tt(P("bs1"), P("bs1"), P("t1"), OP.add)
+                ts(P("bs2"), P("bs2"), P("t2"), 7.0 * ROW, OP.add, OP.add)
+            if rnd == 0 and k == 2:
+                ts(R("sel", 4, 6), R("k2", 0, 2), 16.0, P("bs3"), OP.mult, OP.add)
+                ts(R("sel", 0, 2), R("k2", 0, 2), 16.0, P("bs1"), OP.mult, OP.add)
+            if rnd == 0 and k == 3:
+                ts(P("t1"), P("ph"), 0.0, ROW + 1.0 - 32 - PLAIN, OP.is_equal, OP.mult)
+                ts(P("t2"), P("ph"), 0.0, 15.0, OP.is_gt, OP.mult)
+            if rnd == 0 and k == 4:
+                tt(P("bs2"), P("bs2"), P("t1"), OP.add)
+                ts(P("t2"), P("t2"), 1.0, None, OP.add)
+            if rnd == 0 and k == 5:
+                ts(R("sel", 2, 4), R("k2", 0, 2), P("t2"), P("bs2"), OP.mult, OP.add)
+                memset(R("tr", 8 * ROW, 8 * ROW + 32), 0.0)
+            if not last and k == 6:
+                place("oab", 1, PLAIN)
+            turns(k + 1, name)
+            if k == 6:
+                break
+            off = "ob%d" % k if k < 5 else "oa%d" % k
+            gather("s", "fb", name, off, CFG["nb"])
+            gather("v", "fb", name, off, CFG["nb"])
+            place("oa%d" % (k + 1), k + 1, slot(k + 1), half(k + 1))
+            place("oa%d" % (k + 1), k + 1, slot(k + 1), half(k), half(k + 1))
+            if k < 4:
+                place("ob%d" % (k + 1), k + 1, slot(k + 1), half(k + 1))
+                place("ob%d" % (k + 1), k + 1, slot(k + 3), half(k), half(k + 1))
+            if rnd == 0 and k == 2:
+                ts(R("l0", 0, 32), R("tr", 0, 2 * ROW), float(HALF), None, OP.add, None, R("sel", 4, 6))
+                remote(R("le", 0, 24), R("l0", 0, 24), mate, "are", "loe", topo, core)
+                arrives(R("le", 0, 24), "are", n)
         if last:
-            dma("y", "st", R("lb16", 0, C, 1, 0, 1), R("new", 32, ROW, 1, 0, 1))
-            for k in range(1, 8):
-                dma("y", "st", R("lb16", 0, C, 1, k, k + 1), R("f%d" % k, 32, ROW, 1, 8, 9))
-        else:
-            for s in (0, 7):
-                dma("y", "nb%d" % rnd, R("base", 0, 400, 1, s, 128, 16), R("new", 16, ROW, 1, s, 128, 16))
-        ts(R("lf", 0, 64), full, float(HALF), None, OP.add, None, R("sel", 0, 4))
-        remote(R("lr%d" % rnd, 0, 24), R("lf", 32, 56), mate, "ar%dl" % rnd, "lo%dl" % rnd, topo, core)
-        n = len(topo.engines(mate, core))
+            for k in range(8):
+                p = half(k)[0] + PLAIN
+                dma("y", "st", R("lb16", 0, C, 1, k, k + 1), R("f%d" % max(k, 1), 32, ROW, 1, p, p + 1))
+        copy("v", R("tr", 8 * ROW, 8 * ROW + 25, 1, *half(0)), R("tr", 7 * ROW + 16 + PLAIN, 8 * ROW, 16, *half(1)))
+        ts(R("lz", 0, 32), R("tr", 0, 8 * ROW), float(HALF), None, OP.add, None, R("sel", 0, 2))
+        ts(R("ls", 0, 32), R("tr", 0, 8 * ROW + 32), float(HALF), None, OP.add, None, R("sel", 2, 4))
+        remote(R("lr%d" % rnd, 0, 24), R("ls", 0, 24), mate, "ar%dl" % rnd, "lo%dl" % rnd, topo, core)
         arrives(R("lr%d" % rnd, 0, 24), "ar%dl" % rnd, n)
-        def layer(k):
-            a, b = ZCH[k]
-            for i in (0, 2, 1, 3):
-                mm((4, 0)[k % 2] + i, b - a, "wq", 128 * i, "zq", a)
 
-        def result(k, i):
-            a, b = ZCH[k]
-            src, dst = R("ps%d" % ((4, 0)[k % 2] + i), 0, b - a), R("hp%d" % i, a, b)
-            if i < 2:
+        def layer(k, i):
+            a, b = THIRDS[k]
+            mm(bank(k, i), b - a, "wq", 128 * i, "zq", a)
+
+        def result(k, i, q):
+            a, b = THIRDS[k]
+            src, dst = R("ps%d" % bank(k, i), 0, b - a), R("hp%d" % i, a, b)
+            if q == "v":
                 ts(dst, src, 0.03125, None, OP.mult)
             else:
                 copy("s", dst, src, scale=0.03125)
 
-        def parts(k, t):
-            a, b = SCH[k]
-            copy("vvss"[t], R("hg", 4 * a + t, 4 * b, 4), R("hp%d" % t, 0, C), R("lm" if rnd == 0 else "lr%d" % rnd, a // 16, b // 16))
+        def parts(k, t, q):
+            a, b = sch[k]
+            copy(q, R("hg", 4 * a + t, 4 * b, 4), R("hp%d" % t, 0, C), R("lm" if rnd == 0 else "lr%d" % rnd, a // 16, b // 16))
 
-        def zed(k, t):
-            a, b = ZCH[k]
-            copy("vvss"[t], R("zt", 4 * a + t, 4 * b, 4), R("xp%d" % t, 0, C), R("lf", a // 16, b // 16))
+        def zed(k, t, q):
+            a, b = THIRDS[k]
+            copy(q, R("zt", 4 * a + t, 4 * b, 4), R("xp%d" % t, 0, C), R("lz", a // 16, b // 16))
 
-        for t in range(4):
-            zed(0, t)
-        for k, (a, b) in enumerate(ZCH):
-            if k + 1 < len(ZCH):
-                zed(k + 1, 0)
-                zed(k + 1, 2)
-                zed(k + 1, 3)
-            quant("zq", a, b, "zt", 4 * a)
-            if k + 1 < len(ZCH):
-                zed(k + 1, 1)
-            if k < 2:
-                layer(k)
-        for k in range(len(ZCH) - 1):
-            for i in (0, 2, 1, 3):
-                result(k, i)
-            if k == 0:
-                for j in range(2, len(ZCH)):
-                    layer(j)
-        if rnd == 0:
-            copy("v", R("lm", 0, 24, 1, 96, 128), R("le", 0, 24, 1, 96, 128))
-            copy("v", R("lm", 0, 24, 1, 0, 96), R("lr0", 0, 24, 1, 0, 96))
-        for i in (0, 2, 1, 3):
-            result(len(ZCH) - 1, i)
-        for i in (0, 2, 1, 3):
-            parts(0, i)
-        for k, (a, b) in enumerate(SCH):
-            if k:
-                for t in range(4):
-                    parts(k, t)
+        def send(k):
+            a, b = sch[k]
             quant("hq", a, b, "hg", 4 * a)
             remote(B("hr%d" % rnd, a, b), B("hq", a, b), mate, "ar%dc%d" % (rnd, k), "lo%dc%d" % (rnd, k), topo, core)
             remote(R("hr%ds" % rnd, a, b), R("hqs", a, b), mate, "ar%ds%d" % (rnd, k), "lo%ds%d" % (rnd, k), topo, core)
-        for k, (a, b) in enumerate(SCH):
+
+        def merge():
+            if rnd == 0:
+                copy("v", R("lm", 0, 24, 1, 96, 128), R("le", 0, 24, 1, 96, 128))
+                copy("v", R("lm", 0, 24, 1, 0, 96), R("lr0", 0, 24, 1, 0, 96))
+
+        for w in CFG["p4"].split():
+            x = [int(ch) if ch.isdigit() else ch for ch in w[1:]]
+            if w[0] == "q":
+                quant("zq", *THIRDS[x[0]], "zt", 4 * THIRDS[x[0]][0])
+            else:
+                {"z": zed, "l": layer, "r": result, "p": parts, "h": send, "m": merge}[w[0]](*x)
+        for k, (a, b) in enumerate(sch):
             arrives(R("hr%d" % rnd, a, b), "ar%dc%d" % (rnd, k), n)
             arrives(R("hr%ds" % rnd, a, b), "ar%ds%d" % (rnd, k), n)
         if rnd == 0:
             for b in range(4):
                 quant("e%dq" % b, 0, 128, "e%d" % b, 0)
-            ts(R("ml", 0, 25), R("mi", 0, 25), P("cn"), None, OP.add)
         if rnd == 1:
             quant("vq", 0, 128, "vt", 0)
-        if not last:
-            copy("s", R("newc", 0, 400), R("new", 16, ROW))
-            tt(R("dab", 0, 400), R("new", 16, ROW), R("newc", 0, 400), OP.subtract, R("ml", 0, 25))
-            for s, p in ((0, 0), (7, 64)):
-                for h in (0, 64):
-                    dma("y", "nd%d" % rnd, R("delta", 0, 400, 1, h + s, h + 64, 16), R("dab", 0, 400, 1, p + s, p + 64, 16))
-        else:
+        if last:
             copy("s", R("l32", 0, C, 1, 0, 8), R("lb16", 0, C, 1, 0, 8), bias=float(HALF))
             dma("y", "out", None, R("l32", 0, C, 1, 0, 8), None, T.ll[:, :])
-        for k, (a, b) in enumerate(chunks):
-            for i in range(4):
-                mm((4, 0)[k] + i, HALF, "e%dq" % i, 0, "hr%d" % rnd, a)
-        def grow(k, i):
-            a, b = chunks[k]
-            x = R("xt", 4 * a + i, 4 * b, 4)
-            tt(x, R("ps%d" % ((4, 0)[k] + i), 0, HALF), x, OP.add)
 
-        for i in range(4):
-            grow(0, i)
-        grow(1, 0)
-        for k, (a, b) in enumerate(chunks):
-            if k:
-                for i in range(1, 4):
-                    grow(1, i)
+        def unpack(k, i0=0, i1=4):
+            a, b = sch[k]
+            for i in range(i0, i1):
+                mm(bank(k, i), b - a, "e%dq" % i, 0, "hr%d" % rnd, a)
+
+        def grow(k, i):
+            a, b = sch[k]
+            x = R("xt", 4 * a + i, 4 * b, 4)
+            tt(x, R("ps%d" % bank(k, i), 0, b - a), x, OP.add)
+
+        def finished(k):
+            a, b = sch[k]
             quant("xq", a, b, "xt", 4 * a)
-            if not last:
-                continue
             dma("y", "out", None, B("xq", a, b), None, T.oc[:, 4 * a:4 * b])
-            for i in range(4):
-                dma("y", "out", None, R("xqs", a, b, 1, 32 * i, 32 * i + 4), None, T.osc[4 * i:4 * i + 4, a:b])
-            mm(4 + k, HALF, "vq", 0, "xq", a)
-            copy("s", R("ysb", a, b), R("ps%d" % (4 + k), 0, HALF))
+            mm(bank(k, 0), b - a, "vq", 0, "xq", a)
+            if k == len(sch) - 1:
+                for i in range(4):
+                    dma("ys"[i % 2], "out", None, R("xqs", 0, C, 1, 32 * i, 32 * i + 4), None, T.osc[4 * i:4 * i + 4, :])
+            copy("s", R("ysb", a, b), R("ps%d" % bank(k, 0), 0, b - a))
             dma("s", "out", None, R("ysb", a, b), None, T.y[:, a:b])
-        if not last:
-            for k in range(2):
-                scores(k)
+
+        for w in CFG["p5"].split():
+            x = [int(ch) for ch in w[1:]]
+            if last and w[0] in "nw":
+                continue
+            {"u": unpack, "g": grow, "x": finished if last else scores, "n": minus, "w": plus}[w[0]](*x)
     finish()

@@ -5,14 +5,14 @@ HALF = C // 2
 STEP = [1, 2, 4]
 ROW = 416
 THIRDS = [(0, 128), (128, 256), (256, 384)]
-NCH = [(0, 128), (128, 256), (256, 400)]
 PLAIN = 8
-CFG = {"sch": [(0, HALF), (HALF, C)], "na": 12, "nb": 6, "n0": 8,
-       "p4": "z00v z02s z01v z03s z12s q0 z10v l00 l02 l01 l03 z13s z11v z22s z20v q1 z23s z21v l10 l12 r00s q2 l11 r02s r01v r03v r10s l20 l22 r12s l13 l21 l23 "
-             "r11v m r20v r22s p00v p02s r13s r21v r23s p01v p03s p10v h0 p12s p11v p13s h1",
-       "p5": "u0 u1 g00 g01 g02 g03 g10 x0 g11 g12 g13 n0 x1 w0 w1 n1"}
+CFG = {"sch": THIRDS, "na": 11, "nb": 8, "n0": 8, "sb": (4, 0, 5), "nw": 12, "cut": (192, 192, 192), "tc": 256,
+       "zch": THIRDS,
+       "p4": "z02s a z00v z01v z03s z10v z12s q0 l00 l02 l01 l03 z13s z11v z22s z20v q1 l10 l12 z23s z21v r00s r02s q2 l11 r01s r03s l20 l22 l13 l21 l23 "
+             "r10v r12s r11v m r20v r22s r13s p00v r21s p02s r23v p01v p03s p10v h0 p12s p11v p13s h1",
+       "p5": "u0 u1 g00 g01 g02 g03 x0 s0 g10 g11 g12 g13 n0 x1 s1 w0 w1 n1"}
 
-ONE = ["cb", "cn", "cm", "c32", "phf", "gp", "gm", "gn", "ng", "zb", "bs1", "bs2", "bs3", "t1", "t2"]
+ONE = ["cb", "cn", "cm", "c32", "ph", "gp", "gm", "gn", "bs1", "bs2", "bs3", "t1", "t2", "t3", "t4", "t5"]
 
 SCRATCH = {}
 SEMAPHORES = ["cv", "cs", "ct", "cg", "are", "loe"]
@@ -22,8 +22,8 @@ def _declare():
     def sb(name, cols, dtype):
         SCRATCH[name] = ("sbuf", [128, cols], dtype)
     bf, f32, i32, u16, co, u8 = "bfloat16", "float32", "int32", "uint16", "float8_e4m3fn_x4", "uint8"
-    for n, c in (("xt", 4 * C), ("ut", 512), ("vt", 512), ("zt", 4 * C), ("hg", 4 * C), ("fl", 4 * ROW), ("ones", 512), ("cc", 576), ("sr", 128),
-                 ("e0", 512), ("e1", 512), ("e2", 512), ("e3", 512), ("base", 400), ("tb", 896), ("w1", C), ("w2", C),
+    for n, c in (("xt", 4 * C), ("ut", 512), ("vt", 512), ("zt", 4 * C), ("hg", 4 * C), ("fl", 4 * C), ("ones", 516), ("cc", 512), ("sr", 128),
+                 ("et", 516), ("base", C), ("tb", 896), ("w1", C), ("w2", C),
                  ("new", ROW), ("na", ROW), ("fb", ROW), ("tr", 8 * ROW + 32), ("lb16", C)):
         sb(n, c, bf)
     for b in range(4):
@@ -31,28 +31,27 @@ def _declare():
         sb("hp%d" % b, C, bf)
     for k in range(1, 8):
         sb("f%d" % k, ROW, bf)
-    for n, c in (("vi", 512), ("sw", C), ("ns", C), ("ysb", C), ("l32", C), ("d0", 64), ("d1", 64), ("cr", 64), ("ct", 64), ("dw", 24),
+    for n, c in (("vi", 128), ("kb", 2), ("v2", 128), ("md", 6), ("sw", C), ("ns", C), ("ysb", C), ("l32", C), ("d0", 64), ("d1", 32), ("cr", 160), ("ct", 160), ("dw", 24),
                  ("k2", 2), ("one", len(ONE))):
         sb(n, c, f32)
-    for n, c in (("mti", 24), ("iw", 24), ("b16", 1), ("i15", 1), ("ph", 1), ("mi", 26), ("zi", 512), ("zp", 512)):
+    for n, c in (("mti", 24), ("iw", 24), ("mi", 26), ("zi", 128), ("zp", 128)):
         sb(n, c, i32)
-    for n, c in (("mt16", 24), ("o1", 24), ("o2", 24), ("ou", 8), ("sel", 6), ("oab", 26), ("opi", 26), ("lz", 32), ("ls", 32), ("l0", 32), ("le", 24), ("lm", 24)):
+    for n, c in (("mt16", 24), ("o1", 24), ("o2", 24), ("ou", 8), ("sel", 8), ("lr0", 24), ("lr1", 24), ("lr2", 24), ("oab", 26), ("opi", 32), ("lz", 32), ("ls", 32), ("l0", 32), ("le", 24), ("lm", 24)):
         sb(n, c, u16)
     for k in range(7):
         sb("oa%d" % k, 26, u16)
         sb("ob%d" % k, 26, u16)
-    for n, c in (("xq", C), ("u0q", 128), ("uq", 128), ("vq", 128), ("zq", C), ("hq", C), ("fq", ROW), ("wq", 512), ("cq", 144),
+    for n, c in (("xq", C), ("u0q", 128), ("uq", 128), ("vq", 128), ("zq", C), ("hq", C), ("fq", C), ("wq", 512), ("cq", 128),
                  ("e0q", 128), ("e1q", 128), ("e2q", 128), ("e3q", 128)):
         sb(n, c, co)
         sb(n + "s", c, u8)
     for r in range(3):
-        sb("lr%d" % r, 24, u16)
         sb("hr%d" % r, C, co)
         sb("hr%ds" % r, C, u8)
     for k in range(8):
         SCRATCH["ps%d" % k] = ("psum", [128, 512], f32)
     for r in range(3):
-        for n in ("l", "c0", "s0", "c1", "s1", "c2", "s2"):
+        for n in ("l", "c0", "c1", "c2", "s0", "s1", "s2"):
             SEMAPHORES.append("ar%d%s" % (r, n))
             SEMAPHORES.append("lo%d%s" % (r, n))
     for n in ("x0", "x1", "x2", "mt", "u", "v", "wc", "ws", "mi", "st", "out"):
@@ -152,14 +151,17 @@ def _builder(g, T):
                 g.wait_ge(T.sem[sem], cnt[sem])
                 known["g"][sem] = cnt[sem]
 
-    return ap, issue, remote, arrives, finish
+    def after(q, r):
+        wait(q, deps(q, [r], []))
+
+    return ap, issue, remote, arrives, after, finish
 
 
 def rank_program(g, core, T, topo):
     rank = T.rank_of(core)
     if rank is None:
         return
-    ap, issue, remote, arrives, finish = _builder(g, T)
+    ap, issue, remote, arrives, after, finish = _builder(g, T)
 
     def R(name, c0, c1, cs=1, p0=0, p1=128, ps=1):
         return (name, (c0, c1, cs), (p0, p1, ps), False)
@@ -230,107 +232,132 @@ def rank_program(g, core, T, topo):
         issue("g", lambda e: e.affine_select(ap(out), ap(in_), pattern, OP.is_equal, 0.0, base, mult), [in_], [out])
 
     sch = CFG["sch"]
-    pw, zs = P("ct"), P("ct", c=32)
+    pw, zs, g16, b16, odd = [P("ct", c=32 * k) for k in range(5)]
 
     dma("s", "mt", R("mti", 0, 24), None, T.mt[:, :])
+    dma("y", "u", R("ut", 0, 512), None, T.u[:, :])
     for k, (a, b) in enumerate(sch):
-        dma("y", "x%d" % k, R("xt", 4 * a, 4 * b), None, T.x[:, 4 * a:4 * b])
-    dma("s", "u", R("ut", 0, 512), None, T.u[:, :])
+        dma("sy"[k > 0], "x%d" % k, R("xt", 4 * a, 4 * b), None, T.x[:, 4 * a:4 * b])
 
-    iota(R("vi", 0, 512), [[1, 512]], 512, 0, True)
+    def zero(r, flag=True):
+        iota(r, [[0, len(range(*r[1]))]], 0, 0, flag)
+
+    iota(R("v2", 0, 128), [[2, 128]], 2 * 512 + 1, 0, True)
+    for k in range(2):
+        iota(R("cr", 64 + 32 * k, 96 + 32 * k), [[16, 2], [0, 16]], 0, 1 - k, True)
+    iota(R("vi", 0, 128, 16), [[16, 8]], 512, 0, True)
     iota(R("iw", 0, 24), [[16, 24]], 0, 1)
+    zero(R("mi", 0, 26), False)
     for h in range(2):
-        iota(R("sr", 64 * h, 64 * h + 64), [[0, 2], [64, 2], [2, 16]], -h, 0, True)
-    iota(R("ones", 0, 512), [[0, 512]], 1, 0, True)
-    for b in range(4):
-        select(R("e%d" % b, 0, 512), R("ones", 0, 512), [[1, 512]], -b, -4)
-    memset(R("mi", 0, 26), 0)
+        iota(R("sr", 64 * h, 64 * h + 64), [[0, 4], [2, 16]], -h, 0, True)
+    iota(R("sr", 64, 128, 16), [[0, 4]], 7, 0, True)
+    iota(R("cr", 128, 160), [[0, 16], [400, 2]], 16, 0, True)
+    for t in range(1, 3):
+        zero(R("fl", t, 4 * C, 4))
+    iota(R("base", 0, C), [[1, C]], -HALF, 0, True)
+    zero(R("new", 16 + C, ROW))
+    for name in ["new"] + ["f%d" % k for k in range(1, 8)]:
+        zero(R(name, 0, 16))
+    iota(R("ones", 0, 516), [[0, 516]], 1, 0, True)
+    select(R("et", 0, 516), R("ones", 0, 516), [[1, 516]], -3, -4)
+    memset(R("d1", 0, 32), 0.0)
+    for a, step in ((32, 0.5), (0, 2.0)):
+        memset(R("d0", a, a + 16), step)
+        memset(R("d0", a + 16, a + 17), step ** -15)
+        memset(R("d0", a + 17, a + 32), step)
     for h in range(8):
         o = 1 - h % 2
         dma("y", "mi", R("mi", o, o + 24, 1, 16 * h, 16 * h + 16), None, (T.la, T.lb)[h // 4][:, :])
+    after("y", R("xt", 0, 4 * C))
     dma("y", "wc", ("wq", (0, 512, 1), (0, 128, 1), True), None, T.wc[:, :])
     dma("y", "ws", R("wqs", 0, 512), None, T.ws[:, :])
     dma("y", "v", R("vt", 0, 512), None, T.v[:, :])
-    memset(R("d0", 0, 32), 2.0)
-    memset(R("d0", 32, 64), 0.5)
-    memset(R("d1", 0, 64), 0.0)
-    memset(R("d0", 16, 48, 16), 2.0 ** -15)
-    memset(R("d0", 48, 49), 2.0 ** 15)
-    memset(R("fl", 0, ROW), 0.0)
-    issue("v", lambda e: e.tensor_tensor_scan(ap(R("cr", 0, 64)), ap(R("d0", 0, 64)), ap(R("d1", 0, 64)), 0.5, OP.mult, OP.add),
-          [R("d0", 0, 64), R("d1", 0, 64)], [R("cr", 0, 64)])
-    memset(R("cc", 0, 288), 0.0)
+    def powers(a, first):
+        x, y, z = R("cr", a, a + 32), R("d0", a, a + 32), R("d1", 0, 32)
+        issue("v", lambda e: e.tensor_tensor_scan(ap(x), ap(y), ap(z), first, OP.mult, OP.add), [y, z], [x])
+
+    powers(32, 1.0)
+    powers(0, 0.5)
+    memset(R("tr", 8 * ROW, 8 * ROW + 32), 0.0)
+    for a in range(0, 512, 128):
+        copy("s", R("cc", a, a + 128), R("v2", 0, 128), scale=0.0)
+    turn(R("ct", 32, 64), R("cr", 32, 64))
     memset(R("cr", 9, 32, 16), -512.0)
-    memset(R("cc", 288, 576), 0.0)
-    turn(R("ct", 0, 64), R("cr", 0, 64))
-    for k in range(1, 4):
-        copy("s", R("fl", ROW * k, ROW * (k + 1)), R("fl", 0, ROW))
-    memset(R("new", 0, 16), 0.0)
-    memset(R("f1", 0, 16), 0.0)
-    ts(P("zb"), zs, 0.5, -0.5, OP.mult, OP.add)
-    ts(P("i15"), P("iw"), 15, None, OP.bitwise_and)
-    ts(P("ph"), P("iw"), 4, None, OP.logical_shift_right)
-    ts(R("zi", 0, 512), R("vi", 0, 512), zs, P("zb"), OP.mult, OP.add)
-    ts(P("ng"), P("i15"), 9.0, -1.0, OP.is_lt, OP.mult)
-    ts(P("gp"), P("ph"), 16.0, 512.0, OP.mult, OP.add)
-    ts(R("zp", 0, 512), R("zi", 0, 512), 1, None, OP.bitwise_and)
-    ts(P("gm"), P("ph"), -16.0, 512.0, OP.mult, OP.add)
-    tt(R("dw", 0, 24), R("mti", 0, 24), R("iw", 0, 24), OP.subtract)
-    copy("v", R("tb", 0, 512), R("zp", 0, 512))
+    turn(R("ct", 64, 128), R("cr", 64, 128))
+    ts(R("zi", 0, 128), R("v2", 0, 128), zs, -0.5, OP.mult, OP.add)
+    ts(R("md", 0, 3), R("cr", 32 + 7, 32 + 10), zs, None, OP.is_equal)
+    turn(R("ct", 0, 32), R("cr", 0, 32))
+    for name, of, scale, bias in (("gm", g16, -1.0, 512.0), ("gp", g16, 1.0, 512.0), ("ph", g16, 1 / 16, 0.0), ("cm", g16, -1.0, -1.0),
+                                  ("cb", b16, -1.0, 16.0 + HALF), ("c32", b16, -1.0, 32.0 + PLAIN), ("gn", g16, -1.0, 0.0)):
+        copy("s", P(name), of, None, scale, bias)
+    copy("s", P("cn"), b16, None, 1 / 16, P("cm"))
+    for a, b in THIRDS:
+        copy("s", R("fl", 4 * a + 3, 4 * b, 4), R("v2", 0, 128), scale=0.0)
+    ts(R("zp", 0, 128), R("zi", 0, 128), 1, None, OP.bitwise_and)
+    ts(P("md", c=3), P("md"), P("md", c=1), None, OP.add)
+    ts(R("md", 4, 6), R("md", 0, 2), -1.0, P("md", c=2), OP.mult, OP.add)
+    copy("v", R("tb", 0, 128), R("zp", 0, 128))
+    ts(R("ou", 0, 8), R("vi", 0, 128, 16), -512.0, None, OP.add)
+    ts(P("t3"), P("ph"), 4.0, 16.0, OP.is_lt, OP.mult)
+    ts(P("t4"), P("ph"), 0.0, 16.0, OP.is_gt, OP.mult)
+    for k, (c, sign) in enumerate(((0, 1.0), (1, 1.0), (3, 1.0), (2, -1.0), (4, -1.0), (5, -1.0))):
+        ts(R("tb", 128 * (k + 1), 128 * (k + 2)), R("tb", 0, 128), sign, P("md", c=c), OP.mult, OP.add)
+        if k == 1:
+            tt(R("dw", 0, 24), R("mti", 0, 24), R("iw", 0, 24), OP.subtract)
     ts(R("o1", 0, 24), R("dw", 0, 24), -1.0, P("gm"), OP.mult, OP.add)
     ts(R("o2", 0, 24), R("dw", 0, 24), P("gp"), None, OP.add)
-    copy("s", R("tb", 512, 896), R("tb", 0, C), scale=P("ng"))
     copy("s", R("w1", 0, C), R("tb", 0, 896), R("o1", 0, 24))
-    ts(R("ou", 0, 8), R("vi", 0, 128, 16), -512.0, None, OP.add)
+    copy("s", R("w2", 0, C), R("tb", 0, 896), R("o2", 0, 24))
     quant("u0q", 0, 128, "ut", 0)
+    copy("v", R("mt16", 0, 24), R("mti", 0, 24))
+    ts(P("t1"), P("t3"), b16, P("c32"), OP.is_equal, OP.add)
+    ts(P("t2"), P("t3"), b16, P("c32"), OP.not_equal, OP.add)
+    ts(R("cc", 0, 512, 4), R("sr", 0, 128), P("ph"), pw, OP.is_equal, OP.mult)
     issue("v", lambda e: e.tensor_copy(T.uq[:, 0:128].bitcast(dt.uint32), T.u0q[:, 0:128].bitcast(dt.uint32).indirect(T.ou[:, 0:8])),
           [R("u0q", 0, 128), R("ou", 0, 8)], [R("uq", 0, 128)])
-    copy("s", R("uqs", 0, 128), R("u0qs", 0, 128), R("ou", 0, 8))
+    copy("v", R("uqs", 0, 128), R("u0qs", 0, 128), R("ou", 0, 8))
 
     def bank(k, i):
         return 4 * ((k + 1) % 2) + i
 
-    def scores(k):
-        a, b = sch[k]
+    xch = list(sch)
+
+    def state(k):
+        a, b = xch[k]
         quant("xq", a, b, "xt", 4 * a)
-        mm(bank(k, 0), b - a, "uq", 0, "xq", a)
+
+    def scores(k):
+        a, b = xch[k]
+        mm(CFG["sb"][k], b - a, "uq", 0, "xq", a)
 
     def minus(k):
-        a, b = sch[k]
-        tt(R("ns", a, b), R("ps%d" % bank(k, 0), 0, b - a), R("w2", a, b), OP.mult)
+        a, b = xch[k]
+        tt(R("ns", a, b), R("ps%d" % CFG["sb"][k], 0, b - a), R("w2", a, b), OP.mult)
 
     def plus(k):
-        a, b = sch[k]
-        tt(R("sw", a, b), R("ps%d" % bank(k, 0), 0, b - a), R("w1", a, b), OP.mult)
+        a, b = xch[k]
+        tt(R("sw", a, b), R("ps%d" % CFG["sb"][k], 0, b - a), R("w1", a, b), OP.mult)
 
-    def signed(k):
-        plus(k)
-        minus(k)
-
-    scores(0)
-    copy("v", R("w2", 0, C), R("tb", 0, 896), R("o2", 0, 24))
-    scores(1)
-    copy("v", R("mt16", 0, 24), R("mti", 0, 24))
-    ts(P("b16"), P("iw"), 16, None, OP.bitwise_and)
-    copy("v", P("phf"), P("ph"))
-    memset(R("sr", 64, 128, 32), 7.0)
-    for k in range(len(sch)):
-        if k > 1:
-            scores(k)
-        if k == len(sch) - 1:
-            ts(P("cm"), P("b16"), -16.0 - 512 - HALF, None, OP.add)
-            ts(R("cc", 64, 576, 4), R("sr", 0, 128), P("phf"), pw, OP.is_equal, OP.mult)
-            copy("s", R("base", 0, 400), R("vi", 0, 400), bias=P("cm"))
-        signed(k)
+    for k in range(3):
+        state(k)
+        scores(k)
+        if k == 1:
+            quant("cq", 0, 128, "cc", 0)
+    ts(P("bs1"), P("ph"), 1.0, float(ROW), OP.max, OP.mult)
+    ts(P("bs2"), P("ph"), 6.0, -float(ROW), OP.min, OP.mult)
+    ts(P("t5"), P("t4"), -(ROW - 32.0 - PLAIN) / 16, 8 * ROW - 32.0 - PLAIN, OP.mult, OP.add)
+    copy("s", P("bs3"), P("t2"), None, 1.0, float(ROW))
+    copy("s", P("t3"), P("t4"), None, 15 / 16, 1.0)
+    for call, k in ((plus, 0), (plus, 1), (minus, 0), (plus, 2), (minus, 1), (minus, 2)):
+        call(k)
 
     def half(k):
         return (64 * (k % 2), 64 * (k % 2) + 64)
 
     def gather(q, out, win, off, m):
-        if q == "v":
-            copy("v", R(out, 16, 16 + 16 * m), R(win, 16, ROW), R(off, 0, m))
-        else:
-            copy("s", R(out, 16 + 16 * m, ROW), R(win, 16, ROW), R(off, m, 25))
+        cut = m if m % 2 == 0 else 25 - m
+        a, b = (0, cut) if (q == "v") == (m % 2 == 0) else (cut, 25)
+        copy(q, R(out, 16 + 16 * a, 16 + 16 * b), R(win, 16, ROW), R(off, a, b))
 
     def both(out, win, off, m):
         gather("v", out, win, off, m)
@@ -340,13 +367,14 @@ def rank_program(g, core, T, topo):
         of = of or to
         ts(R(off, 0, 25, 1, *to), R("tr", ROW * k + 16 + slot, ROW * (k + 1), 16, *of), P("cb", *to), None, OP.add)
 
-    def across(k, h, shift=0):
-        o = ROW * k + 16 + PLAIN
-        copy("s", R("tr", o + shift, ROW * (k + 1), 16, *half(h + 1)), R("tr", o, ROW * (k + 1), 16, *half(h)))
+    def across(q, k, h, k0=1):
+        o = ROW * k0 + 16 + PLAIN
+        copy(q, R("tr", o + 1, ROW * (k + 1), 16, *half(h + 1)), R("tr", o, ROW * (k + 1), 16, *half(h)))
 
-    def turns(k, name, cut=HALF):
-        turn(R("tr", ROW * k, ROW * k + cut), R(name, 0, cut))
-        turn(R("tr", ROW * k + cut, ROW * (k + 1)), R(name, cut, ROW))
+    def turns(k, name):
+        cut = CFG["tc"]
+        for a, b in ((0, cut), (cut, ROW))[::-1 if CFG["na"] % 2 else 1]:
+            turn(R("tr", ROW * k + a, ROW * k + b), R(name, a, b))
 
     def slot(k):
         return (k + 1) // 2
@@ -358,89 +386,80 @@ def rank_program(g, core, T, topo):
 
         def flags(k):
             a, b = THIRDS[k]
-            tt(R("fl", 4 * (a + 16), 4 * (b + 16), 4), R("sw", 0, C), R("ns", a, b), OP.is_lt, R("mt16", a // 16, b // 16))
+            tt(R("fl", 4 * a, 4 * b, 4), R("sw", 0, C), R("ns", a, b), OP.is_lt, R("mt16", a // 16, b // 16))
 
         def spread(k):
-            a, b = ((0, 144), (144, 272), (272, ROW))[k]
+            a, b = THIRDS[k]
             quant("fq", a, b, "fl", 4 * a)
-            a, b = NCH[k]
-            mm(1 + k, b - a, "cq", 16, "fq", a, True, False)
-            mm(1 + k, b - a, "cq", 0, "fq", a + 16, False, True)
+            mm(1 + k, b - a, "cq", 0, "fq", a)
 
         def renew(k):
-            a, b = NCH[k]
+            a, b = THIRDS[k]
             tt(R("new", 16 + a, 16 + b), R("ps%d" % (1 + k), 0, b - a), R("base", a, b), OP.add)
 
-        for t in range(4):
+        def planar(t):
             copy("s", R("xp%d" % t, 0, C), R("xt", t, 4 * C, 4))
-        if rnd == 0:
-            quant("cq", 0, 144, "cc", 0)
-            ts(P("cn"), P("b16"), -1.0, 16.0, OP.mult, OP.add)
+
+        def turned(k):
+            a, b = THIRDS[k]
+            turn(R("tr", ROW + a, ROW + b), R("new", 16 + a, 16 + b))
+            b += 32 * (k == 2)
+            turn(R("tr", a, b), R("new", a, b))
+
+        for t in range(4):
+            planar(t)
         flags(0)
         flags(1)
         spread(0)
         flags(2)
         spread(1)
         if rnd == 0:
-            ts(R("oab", 0, 25), R("mi", 0, 25), P("cn"), None, OP.add)
-            ts(P("cb"), P("b16"), -1.0, 208.0, OP.mult, OP.add)
+            copy("v", R("oab", 0, 25), R("mi", 0, 25))
         spread(2)
+        if rnd == 0:
+            turn(R("ct", 128, 160), R("cr", 128, 160))
         renew(0)
         if rnd == 0:
-            ts(P("c32"), P("b16"), -1.0, 32.0 + PLAIN, OP.mult, OP.add)
-            ts(P("gn"), P("ph"), -16.0, None, OP.mult)
-            for k in range(2, 8):
-                copy("s", R("f%d" % k, 0, 16), R("new", 0, 16))
+            ts(R("kb", 0, 2), R("iw", 0, 2), P("cn"), 23.0, OP.add, OP.min)
+            ts(R("k2", 0, 2), R("iw", 0, 2), P("gn"), 23.0, OP.add, OP.min)
+            ts(P("bs1"), P("bs1"), P("t1"), None, OP.add)
+            ts(P("bs2"), P("bs2"), P("t2"), P("t5"), OP.add, OP.add)
         renew(1)
-        turn(R("tr", 0, 128), R("new", 0, 128))
+        if rnd == 0:
+            ts(R("sel", 6, 8), R("kb", 0, 2), 16.0, odd, OP.mult, OP.add)
+        turned(0)
         renew(2)
-        turn(R("tr", 128, 256), R("new", 128, 256))
-        turn(R("tr", 256, ROW), R("new", 256, ROW))
+        turned(1)
+        turned(2)
         gather("s", "na", "new", "oab", CFG["n0"])
         gather("v", "na", "new", "oab", CFG["n0"])
-        place("opi", 0, 0)
-        if rnd == 0:
-            ts(P("t1"), P("ph"), 1.0, P("c32"), OP.is_equal, OP.add)
-            ts(P("t2"), P("ph"), 7.0, P("c32"), OP.is_equal, OP.add)
+        ts(R("opi", 0, 32), R("tr", 0, ROW + C), P("cb"), None, OP.add, None, R("sel", 6, 8))
         both("f1", "na", "opi", CFG["na"])
         if rnd == 0:
-            ts(P("bs1"), P("ph"), 1.0, float(ROW), OP.max, OP.mult)
-            ts(P("bs2"), P("ph"), 6.0, -float(ROW), OP.min, OP.mult)
+            ts(R("sel", 4, 6), R("k2", 0, 2), 16.0, P("bs3"), OP.mult, OP.add)
         turns(1, "f1")
-        if rnd == 0:
-            ts(R("k2", 0, 2), R("iw", 0, 2), P("gn"), 23.0, OP.add, OP.min)
-            ts(P("bs3"), P("t2"), float(ROW), None, OP.add)
         place("ob0", 1, 1, half(0), half(1))
         place("ob0", 1, 1, half(1), half(0))
         place("oa1", 1, 1, half(0), half(1))
         place("oa1", 1, 1, half(1))
         both("fb", "f1", "ob0", CFG["na"])
-        across(1, 0, 1)
-        across(1, 1, 1)
+        if rnd == 0:
+            across("s", 1, 0)
         place("ob1", 1, 1, half(1))
         place("ob1", 1, 2, half(0), half(1))
         for k in range(1, 7):
             name = "f%d" % (k + 1)
             both(name, "fb", "oa%d" % k, CFG["na"])
-            if k > 1:
-                across(k, k)
             if rnd == 0 and k == 1:
-                tt(P("bs1"), P("bs1"), P("t1"), OP.add)
-                ts(P("bs2"), P("bs2"), P("t2"), 7.0 * ROW, OP.add, OP.add)
+                ts(R("l0", 0, 32), R("tr", 0, 2 * ROW), float(HALF), None, OP.add, None, R("sel", 4, 6))
+                remote(R("le", 0, 24), R("l0", 0, 24), mate, "are", "loe", topo, core)
+                arrives(R("le", 0, 24), "are", n)
             if rnd == 0 and k == 2:
-                ts(R("sel", 4, 6), R("k2", 0, 2), 16.0, P("bs3"), OP.mult, OP.add)
-                ts(R("sel", 0, 2), R("k2", 0, 2), 16.0, P("bs1"), OP.mult, OP.add)
+                ts(R("sel", 2, 4), R("k2", 0, 2), P("t3"), P("bs2"), OP.mult, OP.add)
             if rnd == 0 and k == 3:
-                ts(P("t1"), P("ph"), 0.0, ROW + 1.0 - 32 - PLAIN, OP.is_equal, OP.mult)
-                ts(P("t2"), P("ph"), 0.0, 15.0, OP.is_gt, OP.mult)
-            if rnd == 0 and k == 4:
-                tt(P("bs2"), P("bs2"), P("t1"), OP.add)
-                ts(P("t2"), P("t2"), 1.0, None, OP.add)
-            if rnd == 0 and k == 5:
-                ts(R("sel", 2, 4), R("k2", 0, 2), P("t2"), P("bs2"), OP.mult, OP.add)
-                memset(R("tr", 8 * ROW, 8 * ROW + 32), 0.0)
-            if not last and k == 6:
-                place("oab", 1, PLAIN)
+                ts(R("sel", 0, 2), R("k2", 0, 2), 16.0, P("bs1"), OP.mult, OP.add)
+            if k == 6 and not last:
+                ts(R("oab", 0, 25), R("tr", ROW + 16 + PLAIN, 2 * ROW, 16), float(HALF), None, OP.add)
             turns(k + 1, name)
             if k == 6:
                 break
@@ -452,26 +471,37 @@ def rank_program(g, core, T, topo):
             if k < 4:
                 place("ob%d" % (k + 1), k + 1, slot(k + 1), half(k + 1))
                 place("ob%d" % (k + 1), k + 1, slot(k + 3), half(k), half(k + 1))
-            if rnd == 0 and k == 2:
-                ts(R("l0", 0, 32), R("tr", 0, 2 * ROW), float(HALF), None, OP.add, None, R("sel", 4, 6))
-                remote(R("le", 0, 24), R("l0", 0, 24), mate, "are", "loe", topo, core)
-                arrives(R("le", 0, 24), "are", n)
+            else:
+                across("v", k + 1, k + 1)
         if last:
             for k in range(8):
                 p = half(k)[0] + PLAIN
                 dma("y", "st", R("lb16", 0, C, 1, k, k + 1), R("f%d" % max(k, 1), 32, ROW, 1, p, p + 1))
-        copy("v", R("tr", 8 * ROW, 8 * ROW + 25, 1, *half(0)), R("tr", 7 * ROW + 16 + PLAIN, 8 * ROW, 16, *half(1)))
+        copy("s", R("tr", 8 * ROW, 8 * ROW + 25, 1, *half(0)), R("tr", 7 * ROW + 16 + PLAIN, 8 * ROW, 16, *half(1)))
+        def lists():
+            ts(R("ls", 0, 32), R("tr", 0, 8 * ROW + 32), float(HALF), None, OP.add, None, R("sel", 2, 4))
+            remote(R("lr%d" % rnd, 0, 24), R("ls", 0, 24), mate, "ar%dl" % rnd, "lo%dl" % rnd, topo, core)
+            arrives(R("lr%d" % rnd, 0, 24), "ar%dl" % rnd, n)
+
         ts(R("lz", 0, 32), R("tr", 0, 8 * ROW), float(HALF), None, OP.add, None, R("sel", 0, 2))
-        ts(R("ls", 0, 32), R("tr", 0, 8 * ROW + 32), float(HALF), None, OP.add, None, R("sel", 2, 4))
-        remote(R("lr%d" % rnd, 0, 24), R("ls", 0, 24), mate, "ar%dl" % rnd, "lo%dl" % rnd, topo, core)
-        arrives(R("lr%d" % rnd, 0, 24), "ar%dl" % rnd, n)
+        cut = CFG["cut"][rnd]
+        zch, hch = CFG["zch"], [(0, cut), (cut, C)]
+        xch[:] = hch
+
+        def zed(k, t, q):
+            a, b = zch[k]
+            copy(q, R("zt", 4 * a + t, 4 * b, 4), R("xp%d" % t, 0, C), R("lz", a // 16, b // 16))
+
+        def packed(k):
+            a, b = zch[k]
+            quant("zq", a, b, "zt", 4 * a)
 
         def layer(k, i):
-            a, b = THIRDS[k]
+            a, b = zch[k]
             mm(bank(k, i), b - a, "wq", 128 * i, "zq", a)
 
         def result(k, i, q):
-            a, b = THIRDS[k]
+            a, b = zch[k]
             src, dst = R("ps%d" % bank(k, i), 0, b - a), R("hp%d" % i, a, b)
             if q == "v":
                 ts(dst, src, 0.03125, None, OP.mult)
@@ -479,36 +509,31 @@ def rank_program(g, core, T, topo):
                 copy("s", dst, src, scale=0.03125)
 
         def parts(k, t, q):
-            a, b = sch[k]
+            a, b = hch[k]
             copy(q, R("hg", 4 * a + t, 4 * b, 4), R("hp%d" % t, 0, C), R("lm" if rnd == 0 else "lr%d" % rnd, a // 16, b // 16))
 
-        def zed(k, t, q):
-            a, b = THIRDS[k]
-            copy(q, R("zt", 4 * a + t, 4 * b, 4), R("xp%d" % t, 0, C), R("lz", a // 16, b // 16))
-
         def send(k):
-            a, b = sch[k]
+            a, b = hch[k]
             quant("hq", a, b, "hg", 4 * a)
             remote(B("hr%d" % rnd, a, b), B("hq", a, b), mate, "ar%dc%d" % (rnd, k), "lo%dc%d" % (rnd, k), topo, core)
+            arrives(R("hr%d" % rnd, a, b), "ar%dc%d" % (rnd, k), n)
             remote(R("hr%ds" % rnd, a, b), R("hqs", a, b), mate, "ar%ds%d" % (rnd, k), "lo%ds%d" % (rnd, k), topo, core)
+            arrives(R("hr%ds" % rnd, a, b), "ar%ds%d" % (rnd, k), n)
 
         def merge():
             if rnd == 0:
                 copy("v", R("lm", 0, 24, 1, 96, 128), R("le", 0, 24, 1, 96, 128))
                 copy("v", R("lm", 0, 24, 1, 0, 96), R("lr0", 0, 24, 1, 0, 96))
 
-        for w in CFG["p4"].split():
-            x = [int(ch) if ch.isdigit() else ch for ch in w[1:]]
-            if w[0] == "q":
-                quant("zq", *THIRDS[x[0]], "zt", 4 * THIRDS[x[0]][0])
-            else:
-                {"z": zed, "l": layer, "r": result, "p": parts, "h": send, "m": merge}[w[0]](*x)
-        for k, (a, b) in enumerate(sch):
-            arrives(R("hr%d" % rnd, a, b), "ar%dc%d" % (rnd, k), n)
-            arrives(R("hr%ds" % rnd, a, b), "ar%ds%d" % (rnd, k), n)
+        def run(text, calls):
+            for w in text.split():
+                if w[0] in calls:
+                    calls[w[0]](*[int(ch) if ch.isdigit() else ch for ch in w[1:]])
+
+        run(CFG["p4"], {"z": zed, "q": packed, "l": layer, "r": result, "p": parts, "h": send, "m": merge, "a": lists})
         if rnd == 0:
             for b in range(4):
-                quant("e%dq" % b, 0, 128, "e%d" % b, 0)
+                quant("e%dq" % b, 0, 128, "et", 3 - b)
         if rnd == 1:
             quant("vq", 0, 128, "vt", 0)
         if last:
@@ -516,29 +541,27 @@ def rank_program(g, core, T, topo):
             dma("y", "out", None, R("l32", 0, C, 1, 0, 8), None, T.ll[:, :])
 
         def unpack(k, i0=0, i1=4):
-            a, b = sch[k]
+            a, b = hch[k]
             for i in range(i0, i1):
                 mm(bank(k, i), b - a, "e%dq" % i, 0, "hr%d" % rnd, a)
 
         def grow(k, i):
-            a, b = sch[k]
+            a, b = hch[k]
             x = R("xt", 4 * a + i, 4 * b, 4)
             tt(x, R("ps%d" % bank(k, i), 0, b - a), x, OP.add)
 
         def finished(k):
-            a, b = sch[k]
-            quant("xq", a, b, "xt", 4 * a)
+            a, b = xch[k]
             dma("y", "out", None, B("xq", a, b), None, T.oc[:, 4 * a:4 * b])
-            mm(bank(k, 0), b - a, "vq", 0, "xq", a)
-            if k == len(sch) - 1:
+            mm(CFG["sb"][k], b - a, "vq", 0, "xq", a)
+            if k == len(xch) - 1:
                 for i in range(4):
                     dma("ys"[i % 2], "out", None, R("xqs", 0, C, 1, 32 * i, 32 * i + 4), None, T.osc[4 * i:4 * i + 4, :])
-            copy("s", R("ysb", a, b), R("ps%d" % bank(k, 0), 0, b - a))
+            copy("s", R("ysb", a, b), R("ps%d" % CFG["sb"][k], 0, b - a))
             dma("s", "out", None, R("ysb", a, b), None, T.y[:, a:b])
 
-        for w in CFG["p5"].split():
-            x = [int(ch) for ch in w[1:]]
-            if last and w[0] in "nw":
-                continue
-            {"u": unpack, "g": grow, "x": finished if last else scores, "n": minus, "w": plus}[w[0]](*x)
+        calls = {"u": unpack, "g": grow, "x": state, "s": finished if last else scores}
+        if not last:
+            calls.update(n=minus, w=plus)
+        run(CFG["p5"], calls)
     finish()

from concourse.mybir import dt, AluOpType as OP, ActivationFunctionType as AF

C = 384
HALF = C // 2
STEP = [1, 2, 4]
ROW = 416
THIRDS = [(0, 128), (128, 256), (256, 384)]
PLAIN = 8
CFG = {"sch": THIRDS, "na": 11, "nb": 8, "n0": 8, "sb": (4, 0, 5), "nw": 12, "cut": (192, 192, 192), "tc": 256,
       "zch": THIRDS,
       "p4": "z02s a z00v z01v z03s z10v z12s q0 l00 l02 l01 l03 z13s z11v z22s z20v q1 l10 l12 z23s z21v r00s r02s q2 l11 r01s r03s l20 l22 l13 l21 l23 "
             "r10v r12s r11v m r20v r22s r13s p00v r21s p02s r23v p01v p03s p10v h0 p12s p11v p13s h1",
       "p5": "u0 u1 g00 g01 g02 g03 x0 s0 g10 g11 g12 g13 n0 x1 s1 w0 w1 n1"}

ONE = ["cb", "cn", "cm", "c32", "ph", "gp", "gm", "gn", "bs1", "bs2", "bs3", "t1", "t2", "t3", "t4", "t5"]

SCRATCH = {}
SEMAPHORES = ["cv", "cs", "ct", "cg", "are", "loe"]


def _declare():
    def sb(name, cols, dtype):
        SCRATCH[name] = ("sbuf", [128, cols], dtype)
    bf, f32, i32, u16, co, u8 = "bfloat16", "float32", "int32", "uint16", "float8_e4m3fn_x4", "uint8"
    for n, c in (("xt", 4 * C), ("ut", 512), ("vt", 512), ("zt", 4 * C), ("hg", 4 * C), ("fl", 4 * C), ("ones", 516), ("cc", 512), ("sr", 128),
                 ("et", 516), ("base", C), ("tb", 896), ("w1", C), ("w2", C),
                 ("new", ROW), ("na", ROW), ("fb", ROW), ("tr", 8 * ROW + 32), ("lb16", C)):
        sb(n, c, bf)
    for b in range(4):
        sb("xp%d" % b, C, bf)
        sb("hp%d" % b, C, bf)
    for k in range(1, 8):
        sb("f%d" % k, ROW, bf)
    for n, c in (("vi", 128), ("kb", 2), ("v2", 128), ("md", 6), ("sw", C), ("ns", C), ("ysb", C), ("l32", C), ("d0", 64), ("d1", 32), ("cr", 160), ("ct", 160), ("dw", 24),
                 ("k2", 2), ("one", len(ONE))):
        sb(n, c, f32)
    for n, c in (("mti", 24), ("iw", 24), ("mi", 26), ("zi", 128), ("zp", 128)):
        sb(n, c, i32)
    for n, c in (("mt16", 24), ("o1", 24), ("o2", 24), ("ou", 8), ("sel", 8), ("lr0", 24), ("lr1", 24), ("lr2", 24), ("oab", 26), ("opi", 32), ("lz", 32), ("ls", 32), ("l0", 32), ("le", 24), ("lm", 24)):
        sb(n, c, u16)
    for k in range(7):
        sb("oa%d" % k, 26, u16)
        sb("ob%d" % k, 26, u16)
    for n, c in (("xq", C), ("u0q", 128), ("uq", 128), ("vq", 128), ("zq", C), ("hq", C), ("fq", C), ("wq", 512), ("cq", 128),
                 ("e0q", 128), ("e1q", 128), ("e2q", 128), ("e3q", 128)):
        sb(n, c, co)
        sb(n + "s", c, u8)
    for r in range(3):
        sb("hr%d" % r, C, co)
        sb("hr%ds" % r, C, u8)
    for k in range(8):
        SCRATCH["ps%d" % k] = ("psum", [128, 512], f32)
    for r in range(3):
        for n in ("l", "c0", "c1", "c2", "s0", "s1", "s2"):
            SEMAPHORES.append("ar%d%s" % (r, n))
            SEMAPHORES.append("lo%d%s" % (r, n))
    for n in ("x0", "x1", "x2", "mt", "u", "v", "wc", "ws", "mi", "st", "out"):
        SEMAPHORES.append("d_" + n)


_declare()


def _span(a, b, s):
    return slice(a, b) if s == 1 else slice(a, b, s)


def _meet(a0, a1, s, b0, b1, t):
    if a0 >= b1 or b0 >= a1:
        return False
    return not (s == t and s > 1 and (a0 - b0) % s)


def _builder(g, T):
    eng = {"v": g.vector, "s": g.scalar, "t": g.tensor, "g": g, "y": g.sync}
    known = {q: {} for q in eng}
    hist, cnt, closed = {}, {}, set()
    serial = [0]

    def ap(r):
        name, c, p, bits = r
        p = slice(None) if p == (0, 128, 1) else _span(*p)
        a = T[name][p, _span(*c)]
        return a.bitcast(dt.uint8) if bits else a

    def deps(q, reads, writes, matmul=False):
        found = {}
        for refs, w in ((reads, False), (writes, True)):
            for name, c, p, bits in refs:
                psum = name[:2] == "ps"
                for (c2, p2, w2, tok, clk, q2, n) in hist.get(name, ()):
                    if psum:
                        if q2 == q and (q == "t" or not (w or w2)):
                            continue
                    else:
                        if not (w or w2):
                            continue
                        if not (_meet(*c, *c2) and _meet(*p, *p2)):
                            continue
                    found[n] = (tok, clk)
        return [found[n] for n in sorted(found, reverse=True)]

    def wait(q, toks):
        k = known[q]
        for (sem, val), clk in toks:
            if sem in closed or sem[:2] == "d_":
                val = cnt[sem]
                closed.add(sem)
            if k.get(sem, 0) >= val:
                continue
            eng[q].wait_ge(T.sem[sem], val)
            k[sem] = val
            for s2, v2 in clk.items():
                if k.get(s2, 0) < v2:
                    k[s2] = v2

    def note(q, reads, writes, tok):
        serial[0] += 1
        clk = dict(known[q])
        for refs, w in ((reads, False), (writes, True)):
            for name, c, p, bits in refs:
                h = hist.setdefault(name, [])
                if w and name[:2] != "ps":
                    h[:] = [e for e in h if not (c[0] <= e[0][0] and e[0][1] <= c[1] and c[2] == 1 and p == (0, 128, 1))]
                h.append((c, p, w, tok, clk, q, serial[0]))

    def issue(q, fn, reads, writes, sem=None, inc=1):
        wait(q, deps(q, reads, writes))
        sem = sem or "c" + q
        assert sem not in closed, sem
        cnt[sem] = cnt.get(sem, 0) + inc
        fn(eng[q]).then_inc(T.sem[sem], inc)
        note(q, reads, writes, (sem, cnt[sem]))

    def remote(out, src, dst, ars, los, topo, core):
        wait("g", deps("g", [src], []))
        rid, pid, _ = topo.addr(dst)
        n = len(topo.engines(core, dst))
        g.remote_dma(ap(out), ap(src), T.sem[ars], T.sem[los], pid, rid, topo.mask(core, dst))
        cnt[los] = n
        note("g", [src], [], (los, n))

    def arrives(out, sem, n):
        serial[0] += 1
        cnt[sem] = n
        hist.setdefault(out[0], []).append((out[1], out[2], True, (sem, n), {}, "remote", serial[0]))

    def finish():
        for sem in sorted(cnt):
            if known["g"].get(sem, 0) < cnt[sem]:
                g.wait_ge(T.sem[sem], cnt[sem])
                known["g"][sem] = cnt[sem]

    def after(q, r):
        wait(q, deps(q, [r], []))

    return ap, issue, remote, arrives, after, finish


def rank_program(g, core, T, topo):
    rank = T.rank_of(core)
    if rank is None:
        return
    ap, issue, remote, arrives, after, finish = _builder(g, T)

    def R(name, c0, c1, cs=1, p0=0, p1=128, ps=1):
        return (name, (c0, c1, cs), (p0, p1, ps), False)

    def B(name, c0, c1):
        return (name, (c0, c1, 1), (0, 128, 1), True)

    def P(name, p0=0, p1=128, c=0):
        if name in ONE:
            name, c = "one", ONE.index(name)
        return R(name, c, c + 1, 1, p0, p1)

    def dma(q, sem, out, in_, ext_in=None, ext_out=None):
        issue(q, lambda e: e.dma_start(ext_out if ext_out is not None else ap(out), ext_in if ext_in is not None else ap(in_)),
              [in_] if in_ else [], [out] if out else [], "d_" + sem, 16)

    def val(s):
        return ap(s) if isinstance(s, tuple) else s

    def memset(r, c):
        issue("v", lambda e: e.memset(ap(r), c), [], [r])

    def tt(out, a, b, op, off=None):
        def fn(e):
            x = ap(a)
            return e.tensor_tensor(ap(out), x.indirect(ap(off)) if off else x, ap(b), op)
        issue("v", fn, [a, b] + ([off] if off else []), [out])

    def ts(out, a, s1, s2, op0, op1=None, off=None):
        def fn(e):
            x = ap(a)
            x = x.indirect(ap(off)) if off else x
            if op1 is None:
                return e.tensor_scalar(ap(out), x, val(s1), None, op0)
            return e.tensor_scalar(ap(out), x, val(s1), val(s2), op0, op1)
        issue("v", fn, [a] + [s for s in (s1, s2, off) if isinstance(s, tuple)], [out])

    def copy(q, out, a, off=None, scale=None, bias=None):
        def fn(e):
            x = ap(a)
            x = x.indirect(ap(off)) if off else x
            if q == "v":
                return e.tensor_copy(ap(out), x)
            if bias is not None:
                return e.activation(ap(out), x, AF.Identity, bias=val(bias), scale=1.0 if scale is None else val(scale))
            return e.activation(ap(out), x, AF.Copy) if scale is None else e.activation(ap(out), x, AF.Copy, scale=val(scale))
        issue(q, fn, [a] + [r for r in (off, bias, scale) if isinstance(r, tuple)], [out])

    def turn(out, a):
        issue("v", lambda e: e.transpose(ap(out), ap(a)), [a], [out])

    def quant(name, c0, c1, tile, t0):
        q, s, t = R(name, c0, c1), R(name + "s", c0, c1), R(tile, t0, t0 + 4 * (c1 - c0))
        issue("v", lambda e: e.quantize_mx(ap(q), ap(s), ap(t)), [t], [q, s])

    def mm(bank, n, lhs, l0, rhs, c0, start=True, stop=True):
        out = R("ps%d" % bank, 0, n)
        a, sa, b, sb = R(lhs, l0, l0 + 128), R(lhs + "s", l0, l0 + 128), R(rhs, c0, c0 + n), R(rhs + "s", c0, c0 + n)
        issue("t", lambda e: e.matmul_mx(ap(out), ap(a), ap(sa), ap(b), ap(sb), start, stop), [a, sa, b, sb], [out])

    def iota(r, pattern, base, mult, flag=False):
        if flag:
            issue("g", lambda e: e.iota(ap(r), pattern, base, mult, allow_small_or_imprecise_dtypes=True), [], [r])
        else:
            issue("g", lambda e: e.iota(ap(r), pattern, base, mult), [], [r])

    def select(out, in_, pattern, base, mult):
        issue("g", lambda e: e.affine_select(ap(out), ap(in_), pattern, OP.is_equal, 0.0, base, mult), [in_], [out])

    sch = CFG["sch"]
    pw, zs, g16, b16, odd = [P("ct", c=32 * k) for k in range(5)]

    dma("s", "mt", R("mti", 0, 24), None, T.mt[:, :])
    dma("y", "u", R("ut", 0, 512), None, T.u[:, :])
    for k, (a, b) in enumerate(sch):
        dma("sy"[k > 0], "x%d" % k, R("xt", 4 * a, 4 * b), None, T.x[:, 4 * a:4 * b])

    def zero(r, flag=True):
        iota(r, [[0, len(range(*r[1]))]], 0, 0, flag)

    iota(R("v2", 0, 128), [[2, 128]], 2 * 512 + 1, 0, True)
    for k in range(2):
        iota(R("cr", 64 + 32 * k, 96 + 32 * k), [[16, 2], [0, 16]], 0, 1 - k, True)
    iota(R("vi", 0, 128, 16), [[16, 8]], 512, 0, True)
    iota(R("iw", 0, 24), [[16, 24]], 0, 1)
    zero(R("mi", 0, 26), False)
    for h in range(2):
        iota(R("sr", 64 * h, 64 * h + 64), [[0, 4], [2, 16]], -h, 0, True)
    iota(R("sr", 64, 128, 16), [[0, 4]], 7, 0, True)
    iota(R("cr", 128, 160), [[0, 16], [400, 2]], 16, 0, True)
    for t in range(1, 3):
        zero(R("fl", t, 4 * C, 4))
    iota(R("base", 0, C), [[1, C]], -HALF, 0, True)
    zero(R("new", 16 + C, ROW))
    for name in ["new"] + ["f%d" % k for k in range(1, 8)]:
        zero(R(name, 0, 16))
    iota(R("ones", 0, 516), [[0, 516]], 1, 0, True)
    select(R("et", 0, 516), R("ones", 0, 516), [[1, 516]], -3, -4)
    memset(R("d1", 0, 32), 0.0)
    for a, step in ((32, 0.5), (0, 2.0)):
        memset(R("d0", a, a + 16), step)
        memset(R("d0", a + 16, a + 17), step ** -15)
        memset(R("d0", a + 17, a + 32), step)
    for h in range(8):
        o = 1 - h % 2
        dma("y", "mi", R("mi", o, o + 24, 1, 16 * h, 16 * h + 16), None, (T.la, T.lb)[h // 4][:, :])
    after("y", R("xt", 0, 4 * C))
    dma("y", "wc", ("wq", (0, 512, 1), (0, 128, 1), True), None, T.wc[:, :])
    dma("y", "ws", R("wqs", 0, 512), None, T.ws[:, :])
    dma("y", "v", R("vt", 0, 512), None, T.v[:, :])
    def powers(a, first):
        x, y, z = R("cr", a, a + 32), R("d0", a, a + 32), R("d1", 0, 32)
        issue("v", lambda e: e.tensor_tensor_scan(ap(x), ap(y), ap(z), first, OP.mult, OP.add), [y, z], [x])

    powers(32, 1.0)
    powers(0, 0.5)
    memset(R("tr", 8 * ROW, 8 * ROW + 32), 0.0)
    for a in range(0, 512, 128):
        copy("s", R("cc", a, a + 128), R("v2", 0, 128), scale=0.0)
    turn(R("ct", 32, 64), R("cr", 32, 64))
    memset(R("cr", 9, 32, 16), -512.0)
    turn(R("ct", 64, 128), R("cr", 64, 128))
    ts(R("zi", 0, 128), R("v2", 0, 128), zs, -0.5, OP.mult, OP.add)
    ts(R("md", 0, 3), R("cr", 32 + 7, 32 + 10), zs, None, OP.is_equal)
    turn(R("ct", 0, 32), R("cr", 0, 32))
    for name, of, scale, bias in (("gm", g16, -1.0, 512.0), ("gp", g16, 1.0, 512.0), ("ph", g16, 1 / 16, 0.0), ("cm", g16, -1.0, -1.0),
                                  ("cb", b16, -1.0, 16.0 + HALF), ("c32", b16, -1.0, 32.0 + PLAIN), ("gn", g16, -1.0, 0.0)):
        copy("s", P(name), of, None, scale, bias)
    copy("s", P("cn"), b16, None, 1 / 16, P("cm"))
    for a, b in THIRDS:
        copy("s", R("fl", 4 * a + 3, 4 * b, 4), R("v2", 0, 128), scale=0.0)
    ts(R("zp", 0, 128), R("zi", 0, 128), 1, None, OP.bitwise_and)
    ts(P("md", c=3), P("md"), P("md", c=1), None, OP.add)
    ts(R("md", 4, 6), R("md", 0, 2), -1.0, P("md", c=2), OP.mult, OP.add)
    copy("v", R("tb", 0, 128), R("zp", 0, 128))
    ts(R("ou", 0, 8), R("vi", 0, 128, 16), -512.0, None, OP.add)
    ts(P("t3"), P("ph"), 4.0, 16.0, OP.is_lt, OP.mult)
    ts(P("t4"), P("ph"), 0.0, 16.0, OP.is_gt, OP.mult)
    for k, (c, sign) in enumerate(((0, 1.0), (1, 1.0), (3, 1.0), (2, -1.0), (4, -1.0), (5, -1.0))):
        ts(R("tb", 128 * (k + 1), 128 * (k + 2)), R("tb", 0, 128), sign, P("md", c=c), OP.mult, OP.add)
        if k == 1:
            tt(R("dw", 0, 24), R("mti", 0, 24), R("iw", 0, 24), OP.subtract)
    ts(R("o1", 0, 24), R("dw", 0, 24), -1.0, P("gm"), OP.mult, OP.add)
    ts(R("o2", 0, 24), R("dw", 0, 24), P("gp"), None, OP.add)
    copy("s", R("w1", 0, C), R("tb", 0, 896), R("o1", 0, 24))
    copy("s", R("w2", 0, C), R("tb", 0, 896), R("o2", 0, 24))
    quant("u0q", 0, 128, "ut", 0)
    copy("v", R("mt16", 0, 24), R("mti", 0, 24))
    ts(P("t1"), P("t3"), b16, P("c32"), OP.is_equal, OP.add)
    ts(P("t2"), P("t3"), b16, P("c32"), OP.not_equal, OP.add)
    ts(R("cc", 0, 512, 4), R("sr", 0, 128), P("ph"), pw, OP.is_equal, OP.mult)
    issue("v", lambda e: e.tensor_copy(T.uq[:, 0:128].bitcast(dt.uint32), T.u0q[:, 0:128].bitcast(dt.uint32).indirect(T.ou[:, 0:8])),
          [R("u0q", 0, 128), R("ou", 0, 8)], [R("uq", 0, 128)])
    copy("v", R("uqs", 0, 128), R("u0qs", 0, 128), R("ou", 0, 8))

    def bank(k, i):
        return 4 * ((k + 1) % 2) + i

    xch = list(sch)

    def state(k):
        a, b = xch[k]
        quant("xq", a, b, "xt", 4 * a)

    def scores(k):
        a, b = xch[k]
        mm(CFG["sb"][k], b - a, "uq", 0, "xq", a)

    def minus(k):
        a, b = xch[k]
        tt(R("ns", a, b), R("ps%d" % CFG["sb"][k], 0, b - a), R("w2", a, b), OP.mult)

    def plus(k):
        a, b = xch[k]
        tt(R("sw", a, b), R("ps%d" % CFG["sb"][k], 0, b - a), R("w1", a, b), OP.mult)

    for k in range(3):
        state(k)
        scores(k)
        if k == 1:
            quant("cq", 0, 128, "cc", 0)
    ts(P("bs1"), P("ph"), 1.0, float(ROW), OP.max, OP.mult)
    ts(P("bs2"), P("ph"), 6.0, -float(ROW), OP.min, OP.mult)
    ts(P("t5"), P("t4"), -(ROW - 32.0 - PLAIN) / 16, 8 * ROW - 32.0 - PLAIN, OP.mult, OP.add)
    copy("s", P("bs3"), P("t2"), None, 1.0, float(ROW))
    copy("s", P("t3"), P("t4"), None, 15 / 16, 1.0)
    for call, k in ((plus, 0), (plus, 1), (minus, 0), (plus, 2), (minus, 1), (minus, 2)):
        call(k)

    def half(k):
        return (64 * (k % 2), 64 * (k % 2) + 64)

    def gather(q, out, win, off, m):
        cut = m if m % 2 == 0 else 25 - m
        a, b = (0, cut) if (q == "v") == (m % 2 == 0) else (cut, 25)
        copy(q, R(out, 16 + 16 * a, 16 + 16 * b), R(win, 16, ROW), R(off, a, b))

    def both(out, win, off, m):
        gather("v", out, win, off, m)
        gather("s", out, win, off, m)

    def place(off, k, slot, to=(0, 128), of=None):
        of = of or to
        ts(R(off, 0, 25, 1, *to), R("tr", ROW * k + 16 + slot, ROW * (k + 1), 16, *of), P("cb", *to), None, OP.add)

    def across(q, k, h, k0=1):
        o = ROW * k0 + 16 + PLAIN
        copy(q, R("tr", o + 1, ROW * (k + 1), 16, *half(h + 1)), R("tr", o, ROW * (k + 1), 16, *half(h)))

    def turns(k, name):
        cut = CFG["tc"]
        for a, b in ((0, cut), (cut, ROW))[::-1 if CFG["na"] % 2 else 1]:
            turn(R("tr", ROW * k + a, ROW * k + b), R(name, a, b))

    def slot(k):
        return (k + 1) // 2

    for rnd, step in enumerate(STEP):
        mate = T.cores[rank ^ step]
        last = rnd == len(STEP) - 1
        n = len(topo.engines(mate, core))

        def flags(k):
            a, b = THIRDS[k]
            tt(R("fl", 4 * a, 4 * b, 4), R("sw", 0, C), R("ns", a, b), OP.is_lt, R("mt16", a // 16, b // 16))

        def spread(k):
            a, b = THIRDS[k]
            quant("fq", a, b, "fl", 4 * a)
            mm(1 + k, b - a, "cq", 0, "fq", a)

        def renew(k):
            a, b = THIRDS[k]
            tt(R("new", 16 + a, 16 + b), R("ps%d" % (1 + k), 0, b - a), R("base", a, b), OP.add)

        def planar(t):
            copy("s", R("xp%d" % t, 0, C), R("xt", t, 4 * C, 4))

        def turned(k):
            a, b = THIRDS[k]
            turn(R("tr", ROW + a, ROW + b), R("new", 16 + a, 16 + b))
            b += 32 * (k == 2)
            turn(R("tr", a, b), R("new", a, b))

        for t in range(4):
            planar(t)
        flags(0)
        flags(1)
        spread(0)
        flags(2)
        spread(1)
        if rnd == 0:
            copy("v", R("oab", 0, 25), R("mi", 0, 25))
        spread(2)
        if rnd == 0:
            turn(R("ct", 128, 160), R("cr", 128, 160))
        renew(0)
        if rnd == 0:
            ts(R("kb", 0, 2), R("iw", 0, 2), P("cn"), 23.0, OP.add, OP.min)
            ts(R("k2", 0, 2), R("iw", 0, 2), P("gn"), 23.0, OP.add, OP.min)
            ts(P("bs1"), P("bs1"), P("t1"), None, OP.add)
            ts(P("bs2"), P("bs2"), P("t2"), P("t5"), OP.add, OP.add)
        renew(1)
        if rnd == 0:
            ts(R("sel", 6, 8), R("kb", 0, 2), 16.0, odd, OP.mult, OP.add)
        turned(0)
        renew(2)
        turned(1)
        turned(2)
        gather("s", "na", "new", "oab", CFG["n0"])
        gather("v", "na", "new", "oab", CFG["n0"])
        ts(R("opi", 0, 32), R("tr", 0, ROW + C), P("cb"), None, OP.add, None, R("sel", 6, 8))
        both("f1", "na", "opi", CFG["na"])
        if rnd == 0:
            ts(R("sel", 4, 6), R("k2", 0, 2), 16.0, P("bs3"), OP.mult, OP.add)
        turns(1, "f1")
        place("ob0", 1, 1, half(0), half(1))
        place("ob0", 1, 1, half(1), half(0))
        place("oa1", 1, 1, half(0), half(1))
        place("oa1", 1, 1, half(1))
        both("fb", "f1", "ob0", CFG["na"])
        if rnd == 0:
            across("s", 1, 0)
        place("ob1", 1, 1, half(1))
        place("ob1", 1, 2, half(0), half(1))
        for k in range(1, 7):
            name = "f%d" % (k + 1)
            both(name, "fb", "oa%d" % k, CFG["na"])
            if rnd == 0 and k == 1:
                ts(R("l0", 0, 32), R("tr", 0, 2 * ROW), float(HALF), None, OP.add, None, R("sel", 4, 6))
                remote(R("le", 0, 24), R("l0", 0, 24), mate, "are", "loe", topo, core)
                arrives(R("le", 0, 24), "are", n)
            if rnd == 0 and k == 2:
                ts(R("sel", 2, 4), R("k2", 0, 2), P("t3"), P("bs2"), OP.mult, OP.add)
            if rnd == 0 and k == 3:
                ts(R("sel", 0, 2), R("k2", 0, 2), 16.0, P("bs1"), OP.mult, OP.add)
            if k == 6 and not last:
                ts(R("oab", 0, 25), R("tr", ROW + 16 + PLAIN, 2 * ROW, 16), float(HALF), None, OP.add)
            turns(k + 1, name)
            if k == 6:
                break
            off = "ob%d" % k if k < 5 else "oa%d" % k
            gather("s", "fb", name, off, CFG["nb"])
            gather("v", "fb", name, off, CFG["nb"])
            place("oa%d" % (k + 1), k + 1, slot(k + 1), half(k + 1))
            place("oa%d" % (k + 1), k + 1, slot(k + 1), half(k), half(k + 1))
            if k < 4:
                place("ob%d" % (k + 1), k + 1, slot(k + 1), half(k + 1))
                place("ob%d" % (k + 1), k + 1, slot(k + 3), half(k), half(k + 1))
            else:
                across("v", k + 1, k + 1)
        if last:
            for k in range(8):
                p = half(k)[0] + PLAIN
                dma("y", "st", R("lb16", 0, C, 1, k, k + 1), R("f%d" % max(k, 1), 32, ROW, 1, p, p + 1))
        copy("s", R("tr", 8 * ROW, 8 * ROW + 25, 1, *half(0)), R("tr", 7 * ROW + 16 + PLAIN, 8 * ROW, 16, *half(1)))
        def lists():
            ts(R("ls", 0, 32), R("tr", 0, 8 * ROW + 32), float(HALF), None, OP.add, None, R("sel", 2, 4))
            remote(R("lr%d" % rnd, 0, 24), R("ls", 0, 24), mate, "ar%dl" % rnd, "lo%dl" % rnd, topo, core)
            arrives(R("lr%d" % rnd, 0, 24), "ar%dl" % rnd, n)

        ts(R("lz", 0, 32), R("tr", 0, 8 * ROW), float(HALF), None, OP.add, None, R("sel", 0, 2))
        cut = CFG["cut"][rnd]
        zch, hch = CFG["zch"], [(0, cut), (cut, C)]
        xch[:] = hch

        def zed(k, t, q):
            a, b = zch[k]
            copy(q, R("zt", 4 * a + t, 4 * b, 4), R("xp%d" % t, 0, C), R("lz", a // 16, b // 16))

        def packed(k):
            a, b = zch[k]
            quant("zq", a, b, "zt", 4 * a)

        def layer(k, i):
            a, b = zch[k]
            mm(bank(k, i), b - a, "wq", 128 * i, "zq", a)

        def result(k, i, q):
            a, b = zch[k]
            src, dst = R("ps%d" % bank(k, i), 0, b - a), R("hp%d" % i, a, b)
            if q == "v":
                ts(dst, src, 0.03125, None, OP.mult)
            else:
                copy("s", dst, src, scale=0.03125)

        def parts(k, t, q):
            a, b = hch[k]
            copy(q, R("hg", 4 * a + t, 4 * b, 4), R("hp%d" % t, 0, C), R("lm" if rnd == 0 else "lr%d" % rnd, a // 16, b // 16))

        def send(k):
            a, b = hch[k]
            quant("hq", a, b, "hg", 4 * a)
            remote(B("hr%d" % rnd, a, b), B("hq", a, b), mate, "ar%dc%d" % (rnd, k), "lo%dc%d" % (rnd, k), topo, core)
            arrives(R("hr%d" % rnd, a, b), "ar%dc%d" % (rnd, k), n)
            remote(R("hr%ds" % rnd, a, b), R("hqs", a, b), mate, "ar%ds%d" % (rnd, k), "lo%ds%d" % (rnd, k), topo, core)
            arrives(R("hr%ds" % rnd, a, b), "ar%ds%d" % (rnd, k), n)

        def merge():
            if rnd == 0:
                copy("v", R("lm", 0, 24, 1, 96, 128), R("le", 0, 24, 1, 96, 128))
                copy("v", R("lm", 0, 24, 1, 0, 96), R("lr0", 0, 24, 1, 0, 96))

        def run(text, calls):
            for w in text.split():
                if w[0] in calls:
                    calls[w[0]](*[int(ch) if ch.isdigit() else ch for ch in w[1:]])

        run(CFG["p4"], {"z": zed, "q": packed, "l": layer, "r": result, "p": parts, "h": send, "m": merge, "a": lists})
        if rnd == 0:
            for b in range(4):
                quant("e%dq" % b, 0, 128, "et", 3 - b)
        if rnd == 1:
            quant("vq", 0, 128, "vt", 0)
        if last:
            copy("s", R("l32", 0, C, 1, 0, 8), R("lb16", 0, C, 1, 0, 8), bias=float(HALF))
            dma("y", "out", None, R("l32", 0, C, 1, 0, 8), None, T.ll[:, :])

        def unpack(k, i0=0, i1=4):
            a, b = hch[k]
            for i in range(i0, i1):
                mm(bank(k, i), b - a, "e%dq" % i, 0, "hr%d" % rnd, a)

        def grow(k, i):
            a, b = hch[k]
            x = R("xt", 4 * a + i, 4 * b, 4)
            tt(x, R("ps%d" % bank(k, i), 0, b - a), x, OP.add)

        def finished(k):
            a, b = xch[k]
            dma("y", "out", None, B("xq", a, b), None, T.oc[:, 4 * a:4 * b])
            mm(CFG["sb"][k], b - a, "vq", 0, "xq", a)
            if k == len(xch) - 1:
                for i in range(4):
                    dma("ys"[i % 2], "out", None, R("xqs", 0, C, 1, 32 * i, 32 * i + 4), None, T.osc[4 * i:4 * i + 4, :])
            copy("s", R("ysb", a, b), R("ps%d" % CFG["sb"][k], 0, b - a))
            dma("s", "out", None, R("ysb", a, b), None, T.y[:, a:b])

        calls = {"u": unpack, "g": grow, "x": state, "s": finished if last else scores}
        if not last:
            calls.update(n=minus, w=plus)
        run(CFG["p5"], calls)
    finish()
